import numpy as np
import ml_dtypes


def mxq(x, axis, fmt="e4m3"):
    dtype, down = {"e4m3": (ml_dtypes.float8_e4m3fn, 7), "e5m2": (ml_dtypes.float8_e5m2, 14)}[fmt]
    v = np.moveaxis(np.asarray(x, np.float32).astype(ml_dtypes.bfloat16).astype(np.float64), axis, -1)
    blocks = v.reshape(v.shape[:-1] + (-1, 32))
    amax = np.abs(blocks).max(-1, keepdims=True)
    byte = np.maximum(np.where(amax > 0, np.frexp(amax)[1] - 1 + 127, 0) - down, 1)
    scale = np.exp2(byte - 127.0)
    codes = (blocks / scale).astype(np.float32).astype(dtype).astype(np.float64)
    return np.moveaxis((codes * scale).reshape(v.shape), -1, axis)


WIDE = False


def mx_kscale(k):
    if not WIDE:
        return np.ones(k)
    levels = np.array([10, -10, 5, -5, 0])
    if k % 512:
        return np.exp2(np.random.permutation(np.resize(levels, k // 32))).repeat(32)
    a = np.empty((k // 512, 16))
    for p in range(k // 512):
        a[p, :8] = np.random.permutation(np.resize(levels, 8))
        for g in range(8):
            far = levels[np.abs(levels - a[p, g]) >= 10]
            a[p, g + 8] = far[np.random.randint(len(far))]
    return np.exp2(a.ravel()).repeat(32)


def f64(x):
    return np.asarray(x).astype(np.float64)


def striped(idx):
    return np.tile(idx.reshape(-1, 16).T, (8, 1)).astype(np.uint16)


def unstriped(offs):
    return offs[:16].T.reshape(-1).astype(np.int64)


E2M1 = np.array([0.0, 0.5, 1.0, 1.5, 2.0, 3.0, 4.0, 6.0, -0.0, -0.5, -1.0, -1.5, -2.0, -3.0, -4.0, -6.0])


def pack_weight(w, fmt):
    k, n = w.shape
    w = f64(np.asarray(w, np.float32).astype(ml_dtypes.bfloat16)).reshape(k // 32, 32, n)
    amax = np.abs(w).max(1)
    if fmt == "e4m3":
        byte = np.frexp(amax)[1] - 1 + 127 - 7
    else:
        mant, ex = np.frexp(amax / 6.0)
        byte = np.where(mant > 0.5, ex, ex - 1) + 127
    byte = np.clip(np.where(amax > 0, byte, 1), 1, 254)
    scaled = (w * np.exp2(127.0 - byte)[:, None, :]).reshape(k, n).astype(np.float32)
    by_word = np.ascontiguousarray(scaled.reshape(k // 512, 128, 4, n).transpose(0, 1, 3, 2))
    if fmt == "e4m3":
        words = by_word.astype(ml_dtypes.float8_e4m3fn).view(np.uint8)
    else:
        c = by_word.astype(ml_dtypes.float4_e2m1fn).view(np.uint8) & 0xF
        words = (c[..., 0::2] | (c[..., 1::2] << 4)).reshape(k // 512, 128, 2 * n)
    return np.ascontiguousarray(words), np.ascontiguousarray(byte.astype(np.uint8).reshape(k // 512, 16, n))


def unpack_weight(words, scales, fmt):
    g, _, n = scales.shape
    words = np.ascontiguousarray(words).reshape(g, 128, n, -1)
    if fmt == "e4m3":
        vals = words.view(ml_dtypes.float8_e4m3fn).astype(np.float64)
    else:
        nib = np.empty((g, 128, n, 4), np.uint8)
        nib[..., 0::2] = words & 0xF
        nib[..., 1::2] = words >> 4
        vals = E2M1[nib]
    vals = vals * np.repeat(np.exp2(scales.astype(np.float64) - 127.0), 8, axis=1)[..., None]
    return vals.transpose(0, 1, 3, 2).reshape(g * 512, n)


def pack_table4(v):
    words, scales = pack_weight(v, "e2m1")
    g, t = words.shape[0] // 2, v.shape[1]
    words = words.reshape(g, 2, 128, t, 2).transpose(0, 2, 3, 1, 4)
    return np.concatenate([words.reshape(g, -1), scales.reshape(g, -1)], axis=1)


def unpack_table4(tab):
    g, t = tab.shape[0], tab.shape[1] // 544
    words = tab[:, :512 * t].reshape(g, 128, t, 2, 2).transpose(0, 3, 1, 2, 4).reshape(2 * g, 128, 2 * t)
    return unpack_weight(words, tab[:, 512 * t:].reshape(2 * g, 16, t), "e2m1")


def pack_table(v):
    words, scales = pack_weight(v, "e4m3")
    return np.concatenate([words.reshape(words.shape[0], -1), scales.reshape(scales.shape[0], -1)], axis=1)


def unpack_table(tab):
    g, t = tab.shape[0], tab.shape[1] // 528
    return unpack_weight(tab[:, :512 * t].reshape(g, 128, t, 4), tab[:, 512 * t:].reshape(g, 16, t), "e4m3")


def silu(v):
    return v / (1.0 + np.exp(-np.maximum(v, -700.0)))


K, L, M, T, S = 512, 2048, 128, 4096, 1536


def setup_inputs():
    n = np.random.standard_normal
    s1 = mx_kscale(K)[:, None]
    s2 = mx_kscale(L)[:, None]
    p_w4 = pack_weight(n((K, M)) / np.sqrt(K) / s1, "e2m1")
    return {
        "tab": pack_table(n((K, T)) * s1),
        "w4_words": p_w4[0],
        "w4_scales": p_w4[1],
        "tab2": pack_table4(n((L, T)) * s2),
        "u": (n((L, M)) / np.sqrt(L) / s2).astype(np.float32),
        "b": (0.3 * n(128)).astype(np.float32),
        "offs": striped(np.random.permutation(T)[:S]),
        "offs2": striped(np.random.permutation(T)[:S]),
    }


def reference(tab, w4_words, w4_scales, tab2, u, b, offs, offs2):
    tab_ = unpack_table(tab)[:, unstriped(offs)]
    w4_ = unpack_weight(w4_words, w4_scales, "e2m1")
    tab2_ = unpack_table4(tab2)[:, unstriped(offs2)]
    u_ = mxq(f64(u), 0, "e4m3")
    y = tab_.T @ w4_ + tab2_.T @ u_
    return silu(y + f64(b)[None, :])

@@ -1,0 +1,161 @@
+from contextlib import ExitStack
+
+import concourse.mybir as mybir
+from concourse.masks import make_identity
+
+K, L, N, T, S = 512, 2048, 128, 4096, 1536
+FLOPS = 2 * S * N * (K + L)
+
+F32 = mybir.dt.float32
+BF16 = mybir.dt.bfloat16
+I32 = mybir.dt.int32
+U32 = mybir.dt.uint32
+U16 = mybir.dt.uint16
+U8 = mybir.dt.uint8
+FP8X4 = mybir.dt.float8_e4m3fn_x4
+FP4X4 = mybir.dt.float4_e2m1fn_x4
+SILU = mybir.ActivationFunctionType.Silu
+
+P = 128
+WORDS = 512 * T
+SLICE = 512
+COLS = S // 16
+
+
+def tile_list_tab48_tm_silu_kernel(tc, tab, w4_words, w4_scales, tab2, u, b, offs, offs2, out):
+    nc = tc.nc
+    with ExitStack() as ctx:
+        lists = ctx.enter_context(tc.tile_pool(name="lists", bufs=1))
+        keep = ctx.enter_context(tc.tile_pool(name="keep", bufs=1))
+        psum = ctx.enter_context(tc.psum_pool(name="psum", bufs=1))
+
+        list2 = lists.tile([P, COLS], U16, name="list2")
+        list1 = lists.tile([P, COLS], U16, name="list1")
+        win2 = keep.tile([P, T // 4], I32, name="win2")
+        win1 = keep.tile([P, T // 4], I32, name="win1")
+
+        nc.sync.dma_start(list2[:], offs2)
+        for m in range(2):
+            nc.sync.dma_start(
+                out=win2[64 * m : 64 * m + 32, :],
+                in_=tab2[m : m + 1, WORDS:].bitcast(I32).rearrange("o (q c) -> (o q) c", c=T // 4),
+            )
+        nc.vector.memset(win1[:], 0)
+        nc.vector.memset(win2[32:64, :], 0)
+        nc.vector.memset(win2[96:128, :], 0)
+        nc.sync.dma_start(list1[:], offs)
+        scales1 = tab[0:1, WORDS:].bitcast(I32).rearrange("o (q c) -> (o q) c", c=T // 4)
+        for q in range(4):
+            nc.scalar.dma_start(out=win1[32 * q : 32 * q + 4, :], in_=scales1[4 * q : 4 * q + 4, :])
+
+        words = [keep.tile([P, T], I32, name=f"words{m}", tag=f"words{m}") for m in range(2)]
+        raw = keep.tile([P, 4, 4, N], F32, name="raw")
+        nc.sync.dma_start(out=words[0][:], in_=tab2[0:1, :WORDS].bitcast(I32).rearrange("o (p t) -> (o p) t", p=P))
+        nc.sync.dma_start(out=raw[:].rearrange("p a i n -> p a (i n)"), in_=u.rearrange("(a p i) n -> p a (i n)", a=4, i=4))
+        nc.sync.dma_start(out=words[1][:], in_=tab2[1:2, :WORDS].bitcast(I32).rearrange("o (p t) -> (o p) t", p=P))
+
+        planes = [keep.tile([P, S], U8, name=f"plane2_{a}", align_bytes=64) for a in range(4)]
+        for a in range(4):
+            nc.gpsimd.memset(planes[a][:].bitcast(I32), 0)
+        w_codes = keep.tile([P, 2 * N], U8, name="w_codes", align_bytes=64)
+        w_scales = keep.tile([P, N], U8, name="w_scales", align_bytes=64)
+        b_col = keep.tile([P, 1], F32, name="b_col")
+        nc.gpsimd.memset(w_scales[:].bitcast(I32), 0)
+        ident = keep.tile([P, P], F32, name="ident")
+        make_identity(nc, ident[:])
+        warm = keep.tile([P, 1], F32, name="warm")
+        nc.scalar.activation(warm[:], ident[:, 0:1], SILU)
+
+        nc.scalar.dma_start(out=w_codes[:].bitcast(I32), in_=w4_words[0].bitcast(I32))
+        for q in range(4):
+            nc.scalar.dma_start(
+                out=w_scales[32 * q : 32 * q + 4, :].bitcast(I32), in_=w4_scales[0, 4 * q : 4 * q + 4, :].bitcast(I32)
+            )
+        nc.scalar.dma_start(out=b_col[:], in_=b.rearrange("(p o) -> p o", o=1))
+
+        got2 = keep.tile([P, S], U8, name="got2", align_bytes=64)
+        nc.vector.tensor_copy(got2[:], win2[:].bitcast(U8).indirect(list2[:]))
+        for a in range(4):
+            for q in range(4):
+                row = 64 * (a // 2) + 16 * (a % 2) + 4 * q
+                nc.sync.dma_start(
+                    out=planes[a][32 * q : 32 * q + 4, :].bitcast(I32), in_=got2[row : row + 4, :].bitcast(I32)
+                )
+        plane1 = keep.tile([P, S], U8, name="plane1", align_bytes=64)
+        nc.vector.tensor_copy(plane1[:], win1[:].bitcast(U8).indirect(list1[:]))
+
+        grouped = keep.tile([P, 4, N, 4], BF16, name="grouped", align_bytes=64)
+        nc.scalar.copy(out=grouped[:], in_=raw[:].rearrange("p a i n -> p a n i"))
+        u_codes = keep.tile([P, 4 * N], U32, name="u_codes", align_bytes=64)
+        u_scales = keep.tile([P, 4 * N], U8, name="u_scales", align_bytes=64)
+
+        parted = [keep.tile([P, 4 * S], U8, name=f"parted{m}", align_bytes=64) for m in range(2)]
+        got = [keep.tile([P, S], U32, name=f"got_{m}", align_bytes=64) for m in range(2)]
+        codes1 = keep.tile([P, S], U32, name="codes1", align_bytes=64)
+
+        def part(m):
+            nc.vector.tensor_copy(
+                parted[m][:].bitcast(U16).rearrange("p (h j) -> p h j", h=2),
+                got[m][:].bitcast(U16).rearrange("p (j h) -> p h j", h=2),
+            )
+
+        acc = [psum.tile([P, SLICE], F32, name=f"acc{s}") for s in range(3)]
+
+        def pass2(a):
+            for s in range(3):
+                first = (a % 2) * 2 * S + 2 * SLICE * s
+                nc.tensor.matmul_mx(
+                    out=acc[s][:],
+                    lhsT=u_codes[:, N * a : N * (a + 1)].bitcast(FP8X4),
+                    lhsT_scale=u_scales[:, N * a : N * (a + 1)],
+                    rhs=parted[a // 2][:, first : first + 2 * SLICE].bitcast(FP4X4),
+                    rhs_scale=planes[a][:, SLICE * s : SLICE * (s + 1)],
+                    start=(a == 0),
+                    stop=False,
+                )
+
+        def pass1(s):
+            nc.tensor.matmul_mx(
+                out=acc[s][:],
+                lhsT=w_codes[:].bitcast(FP4X4),
+                lhsT_scale=w_scales[:],
+                rhs=codes1[:, SLICE * s : SLICE * (s + 1)].bitcast(FP8X4),
+                rhs_scale=plane1[:, SLICE * s : SLICE * (s + 1)],
+                start=False,
+                stop=True,
+            )
+
+        nc.vector.tensor_copy(got[0][:], words[0][:].bitcast(U32).indirect(list2[:]))
+        nc.vector.quantize_mx(
+            out=u_codes[:].bitcast(FP8X4), scales=u_scales[:], in_=grouped[:].rearrange("p a n i -> p (a n i)")
+        )
+        part(0)
+        nc.vector.tensor_copy(got[1][:], words[1][:].bitcast(U32).indirect(list2[:]))
+        words1 = keep.tile([P, T], I32, name="words_tab", tag="words0")
+        nc.sync.dma_start(out=words1[:], in_=tab[0:1, :WORDS].bitcast(I32).rearrange("o (p t) -> (o p) t", p=P))
+        pass2(0)
+        pass2(1)
+        part(1)
+        pass2(2)
+        pass2(3)
+
+        def finish(s, copy_out):
+            for h in range(2):
+                cols = slice(256 * h, 256 * (h + 1))
+                act = keep.tile([P, 256], F32, name=f"act{s}_{h}")
+                nc.scalar.activation(act[:], acc[s][:, cols], SILU, bias=b_col[:])
+                turned = psum.tile([P, 2, N], F32, name=f"turned{(s % 2)}_{h}")
+                for t in range(2):
+                    nc.tensor.transpose(turned[:, t, :], act[:, 128 * t : 128 * (t + 1)], ident[:])
+                res = keep.tile([P, 2, N], F32, name=f"res{s}_{h}")
+                copy_out(res[:], turned[:])
+                rows = out[SLICE * s + 256 * h : SLICE * s + 256 * (h + 1), :]
+                nc.sync.dma_start(out=rows.rearrange("(t p) n -> p t n", p=P), in_=res[:])
+
+        for s in range(3):
+            nc.vector.tensor_copy(
+                codes1[:, SLICE * s : SLICE * (s + 1)],
+                words1[:].bitcast(U32).indirect(list1[:, SLICE // 16 * s : SLICE // 16 * (s + 1)]),
+            )
+            pass1(s)
+            finish(s, nc.vector.tensor_copy if s == 2 else nc.scalar.copy)

@@ -33,54 +33,51 @@ def tile_list_tab48_tm_silu_kernel(tc, tab, w4_words, w4_scales, tab2, u, b, off
         list1 = lists.tile([P, COLS], U16, name="list1")
         win2 = keep.tile([P, T // 4], I32, name="win2")
         win1 = keep.tile([P, T // 4], I32, name="win1")
+        planes = keep.tile([P, 4 * S], U8, name="planes", align_bytes=64)
+        w_codes = keep.tile([P, 2 * N], U8, name="w_codes", align_bytes=64)
+        w_scales = keep.tile([P, N], U8, name="w_scales", align_bytes=64)
+        b_col = keep.tile([P, 1], F32, name="b_col")
+        words = [keep.tile([P, T], I32, name=f"words{m}") for m in range(2)]
+        words1 = keep.tile([P, T], I32, name="words_tab")
+        raw = keep.tile([P, 4, 4, N], F32, name="raw")
+
+        nc.vector.memset(win1[:], 0)
+        nc.vector.memset(win2[0:32, :], 0)
+        nc.vector.memset(win2[96:128, :], 0)
+        nc.vector.memset(planes[:].bitcast(I32), 0)
+        nc.gpsimd.memset(w_scales[:].bitcast(I32), 0)
 
         nc.sync.dma_start(list2[:], offs2)
         for m in range(2):
             nc.sync.dma_start(
-                out=win2[64 * m : 64 * m + 32, :],
-                in_=tab2[m : m + 1, WORDS:].bitcast(I32).rearrange("o (q c) -> (o q) c", c=T // 4),
+                out=win2[32 + m : 96 : 2, :],
+                in_=tab2[m : m + 1, WORDS:].bitcast(I32).rearrange("o (h q c) -> (o q) h c", h=2, q=16),
             )
-        nc.vector.memset(win1[:], 0)
-        nc.vector.memset(win2[32:64, :], 0)
-        nc.vector.memset(win2[96:128, :], 0)
         nc.sync.dma_start(list1[:], offs)
+        nc.sync.dma_start(out=words[0][:], in_=tab2[0:1, :WORDS].bitcast(I32).rearrange("o (p t) -> (o p) t", p=P))
+        nc.sync.dma_start(out=raw[:].rearrange("p a i n -> p a (i n)"), in_=u.rearrange("(a p i) n -> p a (i n)", a=4, i=4))
+        nc.sync.dma_start(out=words1[:], in_=tab[0:1, :WORDS].bitcast(I32).rearrange("o (p t) -> (o p) t", p=P))
+        nc.sync.dma_start(out=words[1][:], in_=tab2[1:2, :WORDS].bitcast(I32).rearrange("o (p t) -> (o p) t", p=P))
+
         scales1 = tab[0:1, WORDS:].bitcast(I32).rearrange("o (q c) -> (o q) c", c=T // 4)
         for q in range(4):
             nc.scalar.dma_start(out=win1[32 * q : 32 * q + 4, :], in_=scales1[4 * q : 4 * q + 4, :])
-
-        words = [keep.tile([P, T], I32, name=f"words{m}", tag=f"words{m}") for m in range(2)]
-        raw = keep.tile([P, 4, 4, N], F32, name="raw")
-        nc.sync.dma_start(out=words[0][:], in_=tab2[0:1, :WORDS].bitcast(I32).rearrange("o (p t) -> (o p) t", p=P))
-        nc.sync.dma_start(out=raw[:].rearrange("p a i n -> p a (i n)"), in_=u.rearrange("(a p i) n -> p a (i n)", a=4, i=4))
-        nc.sync.dma_start(out=words[1][:], in_=tab2[1:2, :WORDS].bitcast(I32).rearrange("o (p t) -> (o p) t", p=P))
-
-        planes = [keep.tile([P, S], U8, name=f"plane2_{a}", align_bytes=64) for a in range(4)]
-        for a in range(4):
-            nc.gpsimd.memset(planes[a][:].bitcast(I32), 0)
-        w_codes = keep.tile([P, 2 * N], U8, name="w_codes", align_bytes=64)
-        w_scales = keep.tile([P, N], U8, name="w_scales", align_bytes=64)
-        b_col = keep.tile([P, 1], F32, name="b_col")
-        nc.gpsimd.memset(w_scales[:].bitcast(I32), 0)
-        ident = keep.tile([P, P], F32, name="ident")
-        make_identity(nc, ident[:])
-        warm = keep.tile([P, 1], F32, name="warm")
-        nc.scalar.activation(warm[:], ident[:, 0:1], SILU)
-
-        nc.scalar.dma_start(out=w_codes[:].bitcast(I32), in_=w4_words[0].bitcast(I32))
+        nc.gpsimd.dma_start(out=w_codes[:].bitcast(I32), in_=w4_words[0].bitcast(I32))
         for q in range(4):
-            nc.scalar.dma_start(
+            nc.gpsimd.dma_start(
                 out=w_scales[32 * q : 32 * q + 4, :].bitcast(I32), in_=w4_scales[0, 4 * q : 4 * q + 4, :].bitcast(I32)
             )
-        nc.scalar.dma_start(out=b_col[:], in_=b.rearrange("(p o) -> p o", o=1))
+        nc.gpsimd.dma_start(out=b_col[:], in_=b.rearrange("(p o) -> p o", o=1))
+        ident = keep.tile([P, P], F32, name="ident")
+        make_identity(nc, ident[:])
 
         got2 = keep.tile([P, S], U8, name="got2", align_bytes=64)
         nc.vector.tensor_copy(got2[:], win2[:].bitcast(U8).indirect(list2[:]))
-        for a in range(4):
-            for q in range(4):
-                row = 64 * (a // 2) + 16 * (a % 2) + 4 * q
-                nc.sync.dma_start(
-                    out=planes[a][32 * q : 32 * q + 4, :].bitcast(I32), in_=got2[row : row + 4, :].bitcast(I32)
-                )
+        for q in range(4):
+            nc.scalar.dma_start(
+                out=planes[32 * q : 32 * q + 4, :].bitcast(I32).rearrange("r (a c) -> r a c", a=4),
+                in_=got2[32 + 16 * q : 48 + 16 * q, :].bitcast(I32),
+            )
         plane1 = keep.tile([P, S], U8, name="plane1", align_bytes=64)
         nc.vector.tensor_copy(plane1[:], win1[:].bitcast(U8).indirect(list1[:]))
 
@@ -89,30 +86,25 @@ def tile_list_tab48_tm_silu_kernel(tc, tab, w4_words, w4_scales, tab2, u, b, off
         u_codes = keep.tile([P, 4 * N], U32, name="u_codes", align_bytes=64)
         u_scales = keep.tile([P, 4 * N], U8, name="u_scales", align_bytes=64)
 
-        parted = [keep.tile([P, 4 * S], U8, name=f"parted{m}", align_bytes=64) for m in range(2)]
-        got = [keep.tile([P, S], U32, name=f"got_{m}", align_bytes=64) for m in range(2)]
-        codes1 = keep.tile([P, S], U32, name="codes1", align_bytes=64)
-
-        def part(m):
-            nc.vector.tensor_copy(
-                parted[m][:].bitcast(U16).rearrange("p (h j) -> p h j", h=2),
-                got[m][:].bitcast(U16).rearrange("p (j h) -> p h j", h=2),
-            )
-
         acc = [psum.tile([P, SLICE], F32, name=f"acc{s}") for s in range(3)]
 
-        def pass2(a):
-            for s in range(3):
-                first = (a % 2) * 2 * S + 2 * SLICE * s
-                nc.tensor.matmul_mx(
-                    out=acc[s][:],
-                    lhsT=u_codes[:, N * a : N * (a + 1)].bitcast(FP8X4),
-                    lhsT_scale=u_scales[:, N * a : N * (a + 1)],
-                    rhs=parted[a // 2][:, first : first + 2 * SLICE].bitcast(FP4X4),
-                    rhs_scale=planes[a][:, SLICE * s : SLICE * (s + 1)],
-                    start=(a == 0),
-                    stop=False,
-                )
+        def part(dst, src):
+            nc.vector.tensor_copy(
+                dst[:].bitcast(U16).rearrange("p (h j) -> p h j", h=2),
+                src[:].bitcast(U16).rearrange("p (j h) -> p h j", h=2),
+            )
+
+        def pass2(a, s, codes, first):
+            plane = S * (2 * (a % 2) + a // 2) + SLICE * s
+            nc.tensor.matmul_mx(
+                out=acc[s][:],
+                lhsT=u_codes[:, N * a : N * (a + 1)].bitcast(FP8X4),
+                lhsT_scale=u_scales[:, N * a : N * (a + 1)],
+                rhs=codes[:, first : first + 2 * SLICE].bitcast(FP4X4),
+                rhs_scale=planes[:, plane : plane + SLICE],
+                start=(a == 0),
+                stop=(a == 3),
+            )
 
         def pass1(s):
             nc.tensor.matmul_mx(
@@ -122,22 +114,23 @@ def tile_list_tab48_tm_silu_kernel(tc, tab, w4_words, w4_scales, tab2, u, b, off
                 rhs=codes1[:, SLICE * s : SLICE * (s + 1)].bitcast(FP8X4),
                 rhs_scale=plane1[:, SLICE * s : SLICE * (s + 1)],
                 start=False,
-                stop=True,
+                stop=False,
             )
 
-        nc.vector.tensor_copy(got[0][:], words[0][:].bitcast(U32).indirect(list2[:]))
+        got0 = keep.tile([P, S], U32, name="got0", align_bytes=64)
+        parted0 = keep.tile([P, 4 * S], U8, name="parted0", align_bytes=64)
+        codes1 = keep.tile([P, S], U32, name="codes1", align_bytes=64)
+        nc.vector.tensor_copy(got0[:], words[0][:].bitcast(U32).indirect(list2[:]))
+        part(parted0, got0)
         nc.vector.quantize_mx(
             out=u_codes[:].bitcast(FP8X4), scales=u_scales[:], in_=grouped[:].rearrange("p a n i -> p (a n i)")
         )
-        part(0)
-        nc.vector.tensor_copy(got[1][:], words[1][:].bitcast(U32).indirect(list2[:]))
-        words1 = keep.tile([P, T], I32, name="words_tab", tag="words0")
-        nc.sync.dma_start(out=words1[:], in_=tab[0:1, :WORDS].bitcast(I32).rearrange("o (p t) -> (o p) t", p=P))
-        pass2(0)
-        pass2(1)
-        part(1)
-        pass2(2)
-        pass2(3)
+        for a in range(2):
+            for s in range(3):
+                pass2(a, s, parted0, a * 2 * S + 2 * SLICE * s)
+        nc.vector.tensor_copy(codes1[:], words1[:].bitcast(U32).indirect(list1[:]))
+        for s in range(3):
+            pass1(s)
 
         def finish(s, copy_out):
             for h in range(2):
@@ -153,9 +146,12 @@ def tile_list_tab48_tm_silu_kernel(tc, tab, w4_words, w4_scales, tab2, u, b, off
                 nc.sync.dma_start(out=rows.rearrange("(t p) n -> p t n", p=P), in_=res[:])
 
         for s in range(3):
+            got = keep.tile([P, SLICE], U32, name=f"got1_{s}", align_bytes=64)
+            parted = keep.tile([P, 4 * SLICE], U8, name=f"parted1_{s}", align_bytes=64)
             nc.vector.tensor_copy(
-                codes1[:, SLICE * s : SLICE * (s + 1)],
-                words1[:].bitcast(U32).indirect(list1[:, SLICE // 16 * s : SLICE // 16 * (s + 1)]),
+                got[:], words[1][:].bitcast(U32).indirect(list2[:, SLICE // 16 * s : SLICE // 16 * (s + 1)])
             )
-            pass1(s)
+            part(parted, got)
+            for h in range(2):
+                pass2(2 + h, s, parted, h * 2 * SLICE)
             finish(s, nc.vector.tensor_copy if s == 2 else nc.scalar.copy)

@@ -46,6 +46,8 @@ def tile_list_tab48_tm_silu_kernel(tc, tab, w4_words, w4_scales, tab2, u, b, off
         nc.vector.memset(win2[96:128, :], 0)
         nc.vector.memset(planes[:].bitcast(I32), 0)
         nc.gpsimd.memset(w_scales[:].bitcast(I32), 0)
+        ident = keep.tile([P, P], F32, name="ident")
+        make_identity(nc, ident[:])
 
         nc.sync.dma_start(list2[:], offs2)
         for m in range(2):
@@ -55,21 +57,25 @@ def tile_list_tab48_tm_silu_kernel(tc, tab, w4_words, w4_scales, tab2, u, b, off
             )
         nc.sync.dma_start(list1[:], offs)
         nc.sync.dma_start(out=words[0][:], in_=tab2[0:1, :WORDS].bitcast(I32).rearrange("o (p t) -> (o p) t", p=P))
+
+        def load_w_scales(q):
+            nc.sync.dma_start(
+                out=w_scales[32 * q : 32 * q + 4, :].bitcast(I32), in_=w4_scales[0, 4 * q : 4 * q + 4, :].bitcast(I32)
+            )
+
+        nc.sync.dma_start(out=w_codes[:].bitcast(I32), in_=w4_words[0].bitcast(I32))
+        nc.sync.dma_start(out=b_col[:], in_=b.rearrange("(p o) -> p o", o=1))
         nc.sync.dma_start(out=raw[:].rearrange("p a i n -> p a (i n)"), in_=u.rearrange("(a p i) n -> p a (i n)", a=4, i=4))
-        nc.sync.dma_start(out=words1[:], in_=tab[0:1, :WORDS].bitcast(I32).rearrange("o (p t) -> (o p) t", p=P))
+        load_w_scales(0)
+        load_w_scales(1)
         nc.sync.dma_start(out=words[1][:], in_=tab2[1:2, :WORDS].bitcast(I32).rearrange("o (p t) -> (o p) t", p=P))
+        load_w_scales(2)
+        load_w_scales(3)
+        nc.sync.dma_start(out=words1[:], in_=tab[0:1, :WORDS].bitcast(I32).rearrange("o (p t) -> (o p) t", p=P))
 
         scales1 = tab[0:1, WORDS:].bitcast(I32).rearrange("o (q c) -> (o q) c", c=T // 4)
         for q in range(4):
             nc.scalar.dma_start(out=win1[32 * q : 32 * q + 4, :], in_=scales1[4 * q : 4 * q + 4, :])
-        nc.gpsimd.dma_start(out=w_codes[:].bitcast(I32), in_=w4_words[0].bitcast(I32))
-        for q in range(4):
-            nc.gpsimd.dma_start(
-                out=w_scales[32 * q : 32 * q + 4, :].bitcast(I32), in_=w4_scales[0, 4 * q : 4 * q + 4, :].bitcast(I32)
-            )
-        nc.gpsimd.dma_start(out=b_col[:], in_=b.rearrange("(p o) -> p o", o=1))
-        ident = keep.tile([P, P], F32, name="ident")
-        make_identity(nc, ident[:])
 
         got2 = keep.tile([P, S], U8, name="got2", align_bytes=64)
         nc.vector.tensor_copy(got2[:], win2[:].bitcast(U8).indirect(list2[:]))
@@ -80,6 +86,9 @@ def tile_list_tab48_tm_silu_kernel(tc, tab, w4_words, w4_scales, tab2, u, b, off
             )
         plane1 = keep.tile([P, S], U8, name="plane1", align_bytes=64)
         nc.vector.tensor_copy(plane1[:], win1[:].bitcast(U8).indirect(list1[:]))
+
+        warm = keep.tile([P, 1], F32, name="warm")
+        nc.scalar.activation(warm[:], b_col[:], SILU)
 
         grouped = keep.tile([P, 4, N, 4], BF16, name="grouped", align_bytes=64)
         nc.scalar.copy(out=grouped[:], in_=raw[:].rearrange("p a i n -> p a n i"))
@@ -103,7 +112,7 @@ def tile_list_tab48_tm_silu_kernel(tc, tab, w4_words, w4_scales, tab2, u, b, off
                 rhs=codes[:, first : first + 2 * SLICE].bitcast(FP4X4),
                 rhs_scale=planes[:, plane : plane + SLICE],
                 start=(a == 0),
-                stop=(a == 3),
+                stop=False,
             )
 
         def pass1(s):
@@ -114,7 +123,7 @@ def tile_list_tab48_tm_silu_kernel(tc, tab, w4_words, w4_scales, tab2, u, b, off
                 rhs=codes1[:, SLICE * s : SLICE * (s + 1)].bitcast(FP8X4),
                 rhs_scale=plane1[:, SLICE * s : SLICE * (s + 1)],
                 start=False,
-                stop=False,
+                stop=True,
             )
 
         got0 = keep.tile([P, S], U32, name="got0", align_bytes=64)
@@ -128,9 +137,6 @@ def tile_list_tab48_tm_silu_kernel(tc, tab, w4_words, w4_scales, tab2, u, b, off
         for a in range(2):
             for s in range(3):
                 pass2(a, s, parted0, a * 2 * S + 2 * SLICE * s)
-        nc.vector.tensor_copy(codes1[:], words1[:].bitcast(U32).indirect(list1[:]))
-        for s in range(3):
-            pass1(s)
 
         def finish(s, copy_out):
             for h in range(2):
@@ -154,4 +160,11 @@ def tile_list_tab48_tm_silu_kernel(tc, tab, w4_words, w4_scales, tab2, u, b, off
             part(parted, got)
             for h in range(2):
                 pass2(2 + h, s, parted, h * 2 * SLICE)
+
+        for s in range(3):
+            nc.vector.tensor_copy(
+                codes1[:, SLICE * s : SLICE * (s + 1)],
+                words1[:].bitcast(U32).indirect(list1[:, SLICE // 16 * s : SLICE // 16 * (s + 1)]),
+            )
+            pass1(s)
             finish(s, nc.vector.tensor_copy if s == 2 else nc.scalar.copy)

@@ -27,13 +27,13 @@ def tile_list_tab48_tm_silu_kernel(tc, tab, w4_words, w4_scales, tab2, u, b, off
     with ExitStack() as ctx:
         lists = ctx.enter_context(tc.tile_pool(name="lists", bufs=1))
         keep = ctx.enter_context(tc.tile_pool(name="keep", bufs=1))
+        shared = ctx.enter_context(tc.tile_pool(name="shared", bufs=1))
         psum = ctx.enter_context(tc.psum_pool(name="psum", bufs=1))
 
         list2 = lists.tile([P, COLS], U16, name="list2")
         list1 = lists.tile([P, COLS], U16, name="list1")
-        win2 = keep.tile([P, T // 4], I32, name="win2")
-        win1 = keep.tile([P, T // 4], I32, name="win1")
-        planes = keep.tile([P, 4 * S], U8, name="planes", align_bytes=64)
+        win2 = shared.tile([P, T // 4], I32, name="win2", offset=0, align_bytes=64)
+        win1 = shared.tile([P, T // 4], I32, name="win1", offset=T, align_bytes=64)
         w_codes = keep.tile([P, 2 * N], U8, name="w_codes", align_bytes=64)
         w_scales = keep.tile([P, N], U8, name="w_scales", align_bytes=64)
         b_col = keep.tile([P, 1], F32, name="b_col")
@@ -41,17 +41,16 @@ def tile_list_tab48_tm_silu_kernel(tc, tab, w4_words, w4_scales, tab2, u, b, off
         words1 = keep.tile([P, T], I32, name="words_tab")
         raw = keep.tile([P, 4, 4, N], F32, name="raw")
 
-        nc.vector.memset(win1[:], 0)
+        nc.gpsimd.memset(win1[:], 0)
         nc.vector.memset(win2[0:32, :], 0)
         nc.vector.memset(win2[96:128, :], 0)
-        nc.vector.memset(planes[:].bitcast(I32), 0)
         nc.gpsimd.memset(w_scales[:].bitcast(I32), 0)
         ident = keep.tile([P, P], F32, name="ident")
         make_identity(nc, ident[:])
 
         nc.sync.dma_start(list2[:], offs2)
         for m in range(2):
-            nc.sync.dma_start(
+            (nc.sync, nc.scalar)[m].dma_start(
                 out=win2[32 + m : 96 : 2, :],
                 in_=tab2[m : m + 1, WORDS:].bitcast(I32).rearrange("o (h q c) -> (o q) h c", h=2, q=16),
             )
@@ -77,18 +76,19 @@ def tile_list_tab48_tm_silu_kernel(tc, tab, w4_words, w4_scales, tab2, u, b, off
         for q in range(4):
             nc.scalar.dma_start(out=win1[32 * q : 32 * q + 4, :], in_=scales1[4 * q : 4 * q + 4, :])
 
+        warm = keep.tile([P, 1], F32, name="warm")
+        nc.scalar.activation(warm[:], ident[:, 0:1], SILU)
+
         got2 = keep.tile([P, S], U8, name="got2", align_bytes=64)
         nc.vector.tensor_copy(got2[:], win2[:].bitcast(U8).indirect(list2[:]))
+        plane1 = keep.tile([P, S], U8, name="plane1", align_bytes=64)
+        nc.vector.tensor_copy(plane1[:], win1[:].bitcast(U8).indirect(list1[:]))
+        planes = shared.tile([P, 4 * S], U8, name="planes", offset=0, align_bytes=64)
         for q in range(4):
             nc.scalar.dma_start(
                 out=planes[32 * q : 32 * q + 4, :].bitcast(I32).rearrange("r (a c) -> r a c", a=4),
                 in_=got2[32 + 16 * q : 48 + 16 * q, :].bitcast(I32),
             )
-        plane1 = keep.tile([P, S], U8, name="plane1", align_bytes=64)
-        nc.vector.tensor_copy(plane1[:], win1[:].bitcast(U8).indirect(list1[:]))
-
-        warm = keep.tile([P, 1], F32, name="warm")
-        nc.scalar.activation(warm[:], b_col[:], SILU)
 
         grouped = keep.tile([P, 4, N, 4], BF16, name="grouped", align_bytes=64)
         nc.scalar.copy(out=grouped[:], in_=raw[:].rearrange("p a i n -> p a n i"))
@@ -138,18 +138,21 @@ def tile_list_tab48_tm_silu_kernel(tc, tab, w4_words, w4_scales, tab2, u, b, off
             for s in range(3):
                 pass2(a, s, parted0, a * 2 * S + 2 * SLICE * s)
 
-        def finish(s, copy_out):
-            for h in range(2):
-                cols = slice(256 * h, 256 * (h + 1))
-                act = keep.tile([P, 256], F32, name=f"act{s}_{h}")
-                nc.scalar.activation(act[:], acc[s][:, cols], SILU, bias=b_col[:])
-                turned = psum.tile([P, 2, N], F32, name=f"turned{(s % 2)}_{h}")
-                for t in range(2):
+        def finish(s, pieces, copies, stores):
+            width = SLICE // pieces
+            tiles = width // P
+            res = keep.tile([P, 4, N], F32, name=f"res{s}")
+            for h in range(pieces):
+                act = keep.tile([P, width], F32, name=f"act{s}_{h}")
+                nc.scalar.activation(act[:], acc[s][:, width * h : width * (h + 1)], SILU, bias=b_col[:])
+                turned = psum.tile([P, tiles, N], F32, name=f"turned{s}_{h}", tag=f"turned{(s + h) % 5}")
+                for t in range(tiles):
                     nc.tensor.transpose(turned[:, t, :], act[:, 128 * t : 128 * (t + 1)], ident[:])
-                res = keep.tile([P, 2, N], F32, name=f"res{s}_{h}")
-                copy_out(res[:], turned[:])
-                rows = out[SLICE * s + 256 * h : SLICE * s + 256 * (h + 1), :]
-                nc.sync.dma_start(out=rows.rearrange("(t p) n -> p t n", p=P), in_=res[:])
+                copies[h % len(copies)](res[:, tiles * h : tiles * (h + 1), :], turned[:])
+            per = 4 // stores
+            for h in range(stores):
+                rows = out[SLICE * s + P * per * h : SLICE * s + P * per * (h + 1), :]
+                nc.sync.dma_start(out=rows.rearrange("(t p) n -> p t n", p=P), in_=res[:, per * h : per * (h + 1), :])
 
         for s in range(3):
             got = keep.tile([P, SLICE], U32, name=f"got1_{s}", align_bytes=64)
@@ -167,4 +170,6 @@ def tile_list_tab48_tm_silu_kernel(tc, tab, w4_words, w4_scales, tab2, u, b, off
                 words1[:].bitcast(U32).indirect(list1[:, SLICE // 16 * s : SLICE // 16 * (s + 1)]),
             )
             pass1(s)
-            finish(s, nc.vector.tensor_copy if s == 2 else nc.scalar.copy)
+        finish(0, 1, [nc.vector.tensor_copy], 1)
+        finish(1, 1, [nc.vector.tensor_copy], 1)
+        finish(2, 4, [nc.scalar.copy, nc.vector.tensor_copy], 2)

@@ -20,6 +20,8 @@ P = 128
 WORDS = 512 * T
 SLICE = 512
 COLS = S // 16
+LAP = T - 2 * S
+WIN2_AT = 4 * T - LAP
 
 
 def tile_list_tab48_tm_silu_kernel(tc, tab, w4_words, w4_scales, tab2, u, b, offs, offs2, out):
@@ -32,13 +34,16 @@ def tile_list_tab48_tm_silu_kernel(tc, tab, w4_words, w4_scales, tab2, u, b, off
 
         list2 = lists.tile([P, COLS], U16, name="list2")
         list1 = lists.tile([P, COLS], U16, name="list1")
-        win2 = shared.tile([P, T // 4], I32, name="win2", offset=0, align_bytes=64)
-        win1 = shared.tile([P, T // 4], I32, name="win1", offset=T, align_bytes=64)
+        win2 = shared.tile([P, T // 4], I32, name="win2", offset=WIN2_AT, align_bytes=64)
+        win1 = shared.tile([P, T // 4], I32, name="win1", offset=WIN2_AT + T, align_bytes=64)
         w_codes = keep.tile([P, 2 * N], U8, name="w_codes", align_bytes=64)
         w_scales = keep.tile([P, N], U8, name="w_scales", align_bytes=64)
         b_col = keep.tile([P, 1], F32, name="b_col")
-        words = [keep.tile([P, T], I32, name=f"words{m}") for m in range(2)]
-        words1 = keep.tile([P, T], I32, name="words_tab")
+        words0 = keep.tile([P, T], I32, name="words0")
+        seed = keep.tile([P, 1], F32, name="seed")
+        warm = keep.tile([P, 1], F32, name="warm")
+        nc.gpsimd.memset(seed[:], 0.0)
+        nc.scalar.activation(warm[:], seed[:], SILU)
         raw = keep.tile([P, 4, 4, N], F32, name="raw")
 
         nc.gpsimd.memset(win1[:], 0)
@@ -50,40 +55,33 @@ def tile_list_tab48_tm_silu_kernel(tc, tab, w4_words, w4_scales, tab2, u, b, off
 
         nc.sync.dma_start(list2[:], offs2)
         for m in range(2):
-            (nc.sync, nc.scalar)[m].dma_start(
+            nc.sync.dma_start(
                 out=win2[32 + m : 96 : 2, :],
                 in_=tab2[m : m + 1, WORDS:].bitcast(I32).rearrange("o (h q c) -> (o q) h c", h=2, q=16),
             )
         nc.sync.dma_start(list1[:], offs)
-        nc.sync.dma_start(out=words[0][:], in_=tab2[0:1, :WORDS].bitcast(I32).rearrange("o (p t) -> (o p) t", p=P))
-
-        def load_w_scales(q):
-            nc.sync.dma_start(
-                out=w_scales[32 * q : 32 * q + 4, :].bitcast(I32), in_=w4_scales[0, 4 * q : 4 * q + 4, :].bitcast(I32)
-            )
-
         nc.sync.dma_start(out=w_codes[:].bitcast(I32), in_=w4_words[0].bitcast(I32))
         nc.sync.dma_start(out=b_col[:], in_=b.rearrange("(p o) -> p o", o=1))
+        nc.sync.dma_start(out=words0[:], in_=tab2[0:1, :WORDS].bitcast(I32).rearrange("o (p t) -> (o p) t", p=P))
         nc.sync.dma_start(out=raw[:].rearrange("p a i n -> p a (i n)"), in_=u.rearrange("(a p i) n -> p a (i n)", a=4, i=4))
-        load_w_scales(0)
-        load_w_scales(1)
-        nc.sync.dma_start(out=words[1][:], in_=tab2[1:2, :WORDS].bitcast(I32).rearrange("o (p t) -> (o p) t", p=P))
-        load_w_scales(2)
-        load_w_scales(3)
-        nc.sync.dma_start(out=words1[:], in_=tab[0:1, :WORDS].bitcast(I32).rearrange("o (p t) -> (o p) t", p=P))
 
         scales1 = tab[0:1, WORDS:].bitcast(I32).rearrange("o (q c) -> (o q) c", c=T // 4)
         for q in range(4):
             nc.scalar.dma_start(out=win1[32 * q : 32 * q + 4, :], in_=scales1[4 * q : 4 * q + 4, :])
-
-        warm = keep.tile([P, 1], F32, name="warm")
-        nc.scalar.activation(warm[:], ident[:, 0:1], SILU)
+        for q in range(4):
+            nc.scalar.dma_start(
+                out=w_scales[32 * q : 32 * q + 4, :].bitcast(I32), in_=w4_scales[0, 4 * q : 4 * q + 4, :].bitcast(I32)
+            )
 
         got2 = keep.tile([P, S], U8, name="got2", align_bytes=64)
         nc.vector.tensor_copy(got2[:], win2[:].bitcast(U8).indirect(list2[:]))
+        words2 = shared.tile([P, T], I32, name="words2", offset=0, align_bytes=64)
+        nc.sync.dma_start(out=words2[:], in_=tab2[1:2, :WORDS].bitcast(I32).rearrange("o (p t) -> (o p) t", p=P))
         plane1 = keep.tile([P, S], U8, name="plane1", align_bytes=64)
         nc.vector.tensor_copy(plane1[:], win1[:].bitcast(U8).indirect(list1[:]))
-        planes = shared.tile([P, 4 * S], U8, name="planes", offset=0, align_bytes=64)
+        words1 = shared.tile([P, T], I32, name="words_tab", offset=WIN2_AT + 2 * T - LAP, align_bytes=64)
+        nc.sync.dma_start(out=words1[:], in_=tab[0:1, :WORDS].bitcast(I32).rearrange("o (p t) -> (o p) t", p=P))
+        planes = shared.tile([P, 4 * S], U8, name="planes", offset=WIN2_AT + LAP, align_bytes=64)
         for q in range(4):
             nc.scalar.dma_start(
                 out=planes[32 * q : 32 * q + 4, :].bitcast(I32).rearrange("r (a c) -> r a c", a=4),
@@ -129,7 +127,7 @@ def tile_list_tab48_tm_silu_kernel(tc, tab, w4_words, w4_scales, tab2, u, b, off
         got0 = keep.tile([P, S], U32, name="got0", align_bytes=64)
         parted0 = keep.tile([P, 4 * S], U8, name="parted0", align_bytes=64)
         codes1 = keep.tile([P, S], U32, name="codes1", align_bytes=64)
-        nc.vector.tensor_copy(got0[:], words[0][:].bitcast(U32).indirect(list2[:]))
+        nc.vector.tensor_copy(got0[:], words0[:].bitcast(U32).indirect(list2[:]))
         part(parted0, got0)
         nc.vector.quantize_mx(
             out=u_codes[:].bitcast(FP8X4), scales=u_scales[:], in_=grouped[:].rearrange("p a n i -> p (a n i)")
@@ -158,7 +156,7 @@ def tile_list_tab48_tm_silu_kernel(tc, tab, w4_words, w4_scales, tab2, u, b, off
             got = keep.tile([P, SLICE], U32, name=f"got1_{s}", align_bytes=64)
             parted = keep.tile([P, 4 * SLICE], U8, name=f"parted1_{s}", align_bytes=64)
             nc.vector.tensor_copy(
-                got[:], words[1][:].bitcast(U32).indirect(list2[:, SLICE // 16 * s : SLICE // 16 * (s + 1)])
+                got[:], words2[:].bitcast(U32).indirect(list2[:, SLICE // 16 * s : SLICE // 16 * (s + 1)])
             )
             part(parted, got)
             for h in range(2):

@@ -21,7 +21,7 @@ WORDS = 512 * T
 SLICE = 512
 COLS = S // 16
 LAP = T - 2 * S
-WIN2_AT = 4 * T - LAP
+WIN2_AT = 4 * T - LAP // 2
 
 
 def tile_list_tab48_tm_silu_kernel(tc, tab, w4_words, w4_scales, tab2, u, b, offs, offs2, out):
@@ -36,20 +36,14 @@ def tile_list_tab48_tm_silu_kernel(tc, tab, w4_words, w4_scales, tab2, u, b, off
         list1 = lists.tile([P, COLS], U16, name="list1")
         win2 = shared.tile([P, T // 4], I32, name="win2", offset=WIN2_AT, align_bytes=64)
         win1 = shared.tile([P, T // 4], I32, name="win1", offset=WIN2_AT + T, align_bytes=64)
-        w_codes = keep.tile([P, 2 * N], U8, name="w_codes", align_bytes=64)
-        w_scales = keep.tile([P, N], U8, name="w_scales", align_bytes=64)
-        b_col = keep.tile([P, 1], F32, name="b_col")
-        words0 = keep.tile([P, T], I32, name="words0")
-        seed = keep.tile([P, 1], F32, name="seed")
-        warm = keep.tile([P, 1], F32, name="warm")
+        seed = keep.tile([P, 1], F32, name="seed", tag="words0")
+        warm = keep.tile([P, 1], F32, name="warm", tag="raw")
         nc.gpsimd.memset(seed[:], 0.0)
         nc.scalar.activation(warm[:], seed[:], SILU)
-        raw = keep.tile([P, 4, 4, N], F32, name="raw")
 
         nc.gpsimd.memset(win1[:], 0)
         nc.vector.memset(win2[0:32, :], 0)
         nc.vector.memset(win2[96:128, :], 0)
-        nc.gpsimd.memset(w_scales[:].bitcast(I32), 0)
         ident = keep.tile([P, P], F32, name="ident")
         make_identity(nc, ident[:])
 
@@ -60,30 +54,34 @@ def tile_list_tab48_tm_silu_kernel(tc, tab, w4_words, w4_scales, tab2, u, b, off
                 in_=tab2[m : m + 1, WORDS:].bitcast(I32).rearrange("o (h q c) -> (o q) h c", h=2, q=16),
             )
         nc.sync.dma_start(list1[:], offs)
-        nc.sync.dma_start(out=w_codes[:].bitcast(I32), in_=w4_words[0].bitcast(I32))
-        nc.sync.dma_start(out=b_col[:], in_=b.rearrange("(p o) -> p o", o=1))
+        scales1 = tab[0:1, WORDS:].bitcast(I32).rearrange("o (q c) -> (o q) c", c=T // 4)
+        for q in (0, 2, 1, 3):
+            nc.sync.dma_start(out=win1[32 * q : 32 * q + 4, :], in_=scales1[4 * q : 4 * q + 4, :])
+        words0 = keep.tile([P, T], I32, name="words0", tag="words0")
+        raw = keep.tile([P, 4, 4, N], F32, name="raw", tag="raw")
         nc.sync.dma_start(out=words0[:], in_=tab2[0:1, :WORDS].bitcast(I32).rearrange("o (p t) -> (o p) t", p=P))
         nc.sync.dma_start(out=raw[:].rearrange("p a i n -> p a (i n)"), in_=u.rearrange("(a p i) n -> p a (i n)", a=4, i=4))
-
-        scales1 = tab[0:1, WORDS:].bitcast(I32).rearrange("o (q c) -> (o q) c", c=T // 4)
-        for q in range(4):
-            nc.scalar.dma_start(out=win1[32 * q : 32 * q + 4, :], in_=scales1[4 * q : 4 * q + 4, :])
-        for q in range(4):
-            nc.scalar.dma_start(
-                out=w_scales[32 * q : 32 * q + 4, :].bitcast(I32), in_=w4_scales[0, 4 * q : 4 * q + 4, :].bitcast(I32)
-            )
 
         got2 = keep.tile([P, S], U8, name="got2", align_bytes=64)
         nc.vector.tensor_copy(got2[:], win2[:].bitcast(U8).indirect(list2[:]))
         words2 = shared.tile([P, T], I32, name="words2", offset=0, align_bytes=64)
         nc.sync.dma_start(out=words2[:], in_=tab2[1:2, :WORDS].bitcast(I32).rearrange("o (p t) -> (o p) t", p=P))
+        w_codes = shared.tile([P, 2 * N], U8, name="w_codes", offset=4 * T, align_bytes=64)
+        w_scales = shared.tile([P, N], U8, name="w_scales", offset=4 * T + 2 * N, align_bytes=64)
+        b_col = shared.tile([P, 1], F32, name="b_col", offset=4 * T + 3 * N, align_bytes=64)
+        nc.sync.dma_start(out=w_codes[:].bitcast(I32), in_=w4_words[0].bitcast(I32))
+        nc.sync.dma_start(out=b_col[:], in_=b.rearrange("(p o) -> p o", o=1))
+        for q in range(4):
+            nc.sync.dma_start(
+                out=w_scales[32 * q : 32 * q + 4, :].bitcast(I32), in_=w4_scales[0, 4 * q : 4 * q + 4, :].bitcast(I32)
+            )
         plane1 = keep.tile([P, S], U8, name="plane1", align_bytes=64)
         nc.vector.tensor_copy(plane1[:], win1[:].bitcast(U8).indirect(list1[:]))
         words1 = shared.tile([P, T], I32, name="words_tab", offset=WIN2_AT + 2 * T - LAP, align_bytes=64)
         nc.sync.dma_start(out=words1[:], in_=tab[0:1, :WORDS].bitcast(I32).rearrange("o (p t) -> (o p) t", p=P))
         planes = shared.tile([P, 4 * S], U8, name="planes", offset=WIN2_AT + LAP, align_bytes=64)
-        for q in range(4):
-            nc.scalar.dma_start(
+        for q in (0, 2, 1, 3):
+            nc.gpsimd.dma_start(
                 out=planes[32 * q : 32 * q + 4, :].bitcast(I32).rearrange("r (a c) -> r a c", a=4),
                 in_=got2[32 + 16 * q : 48 + 16 * q, :].bitcast(I32),
             )

@@ -64,8 +64,6 @@ def tile_list_tab48_tm_silu_kernel(tc, tab, w4_words, w4_scales, tab2, u, b, off
 
         got2 = keep.tile([P, S], U8, name="got2", align_bytes=64)
         nc.vector.tensor_copy(got2[:], win2[:].bitcast(U8).indirect(list2[:]))
-        words2 = shared.tile([P, T], I32, name="words2", offset=0, align_bytes=64)
-        nc.sync.dma_start(out=words2[:], in_=tab2[1:2, :WORDS].bitcast(I32).rearrange("o (p t) -> (o p) t", p=P))
         w_codes = shared.tile([P, 2 * N], U8, name="w_codes", offset=4 * T, align_bytes=64)
         w_scales = shared.tile([P, N], U8, name="w_scales", offset=4 * T + 2 * N, align_bytes=64)
         b_col = shared.tile([P, 1], F32, name="b_col", offset=4 * T + 3 * N, align_bytes=64)
@@ -75,16 +73,19 @@ def tile_list_tab48_tm_silu_kernel(tc, tab, w4_words, w4_scales, tab2, u, b, off
             nc.sync.dma_start(
                 out=w_scales[32 * q : 32 * q + 4, :].bitcast(I32), in_=w4_scales[0, 4 * q : 4 * q + 4, :].bitcast(I32)
             )
+        words2 = shared.tile([P, T], I32, name="words2", offset=0, align_bytes=64)
+        nc.sync.dma_start(out=words2[:], in_=tab2[1:2, :WORDS].bitcast(I32).rearrange("o (p t) -> (o p) t", p=P))
         plane1 = keep.tile([P, S], U8, name="plane1", align_bytes=64)
         nc.vector.tensor_copy(plane1[:], win1[:].bitcast(U8).indirect(list1[:]))
-        words1 = shared.tile([P, T], I32, name="words_tab", offset=WIN2_AT + 2 * T - LAP, align_bytes=64)
-        nc.sync.dma_start(out=words1[:], in_=tab[0:1, :WORDS].bitcast(I32).rearrange("o (p t) -> (o p) t", p=P))
         planes = shared.tile([P, 4 * S], U8, name="planes", offset=WIN2_AT + LAP, align_bytes=64)
         for q in (0, 2, 1, 3):
-            nc.gpsimd.dma_start(
+            nc.sync.dma_start(
                 out=planes[32 * q : 32 * q + 4, :].bitcast(I32).rearrange("r (a c) -> r a c", a=4),
                 in_=got2[32 + 16 * q : 48 + 16 * q, :].bitcast(I32),
             )
+
+        words1 = shared.tile([P, T], I32, name="words_tab", offset=WIN2_AT + 2 * T - LAP, align_bytes=64)
+        nc.sync.dma_start(out=words1[:], in_=tab[0:1, :WORDS].bitcast(I32).rearrange("o (p t) -> (o p) t", p=P))
 
         grouped = keep.tile([P, 4, N, 4], BF16, name="grouped", align_bytes=64)
         nc.scalar.copy(out=grouped[:], in_=raw[:].rearrange("p a i n -> p a n i"))

@@ -20,8 +20,11 @@ P = 128
 WORDS = 512 * T
 SLICE = 512
 COLS = S // 16
-LAP = T - 2 * S
-WIN2_AT = 4 * T - LAP // 2
+PLANE1_AT = 4 * S
+TAB_AT = 2 * T
+PAIR1_AT = TAB_AT + 4 * T
+SMALL_AT = PAIR1_AT + 4 * T
+WIN2_AT = SMALL_AT - 512
 
 
 def tile_list_tab48_tm_silu_kernel(tc, tab, w4_words, w4_scales, tab2, u, b, offs, offs2, out):
@@ -35,8 +38,8 @@ def tile_list_tab48_tm_silu_kernel(tc, tab, w4_words, w4_scales, tab2, u, b, off
         list2 = lists.tile([P, COLS], U16, name="list2")
         list1 = lists.tile([P, COLS], U16, name="list1")
         win2 = shared.tile([P, T // 4], I32, name="win2", offset=WIN2_AT, align_bytes=64)
-        win1 = shared.tile([P, T // 4], I32, name="win1", offset=WIN2_AT + T, align_bytes=64)
-        seed = keep.tile([P, 1], F32, name="seed", tag="words0")
+        win1 = keep.tile([P, T // 4], I32, name="win1")
+        seed = keep.tile([P, 1], F32, name="seed")
         warm = keep.tile([P, 1], F32, name="warm", tag="raw")
         nc.gpsimd.memset(seed[:], 0.0)
         nc.scalar.activation(warm[:], seed[:], SILU)
@@ -53,46 +56,54 @@ def tile_list_tab48_tm_silu_kernel(tc, tab, w4_words, w4_scales, tab2, u, b, off
                 out=win2[32 + m : 96 : 2, :],
                 in_=tab2[m : m + 1, WORDS:].bitcast(I32).rearrange("o (h q c) -> (o q) h c", h=2, q=16),
             )
+        words0 = shared.tile([P, T], I32, name="words0", offset=0, align_bytes=64)
+        nc.sync.dma_start(out=words0[:], in_=tab2[0:1, :WORDS].bitcast(I32).rearrange("o (p t) -> (o p) t", p=P))
         nc.sync.dma_start(list1[:], offs)
         scales1 = tab[0:1, WORDS:].bitcast(I32).rearrange("o (q c) -> (o q) c", c=T // 4)
         for q in (0, 2, 1, 3):
             nc.sync.dma_start(out=win1[32 * q : 32 * q + 4, :], in_=scales1[4 * q : 4 * q + 4, :])
-        words0 = keep.tile([P, T], I32, name="words0", tag="words0")
         raw = keep.tile([P, 4, 4, N], F32, name="raw", tag="raw")
-        nc.sync.dma_start(out=words0[:], in_=tab2[0:1, :WORDS].bitcast(I32).rearrange("o (p t) -> (o p) t", p=P))
         nc.sync.dma_start(out=raw[:].rearrange("p a i n -> p a (i n)"), in_=u.rearrange("(a p i) n -> p a (i n)", a=4, i=4))
 
         got2 = keep.tile([P, S], U8, name="got2", align_bytes=64)
         nc.vector.tensor_copy(got2[:], win2[:].bitcast(U8).indirect(list2[:]))
-        w_codes = shared.tile([P, 2 * N], U8, name="w_codes", offset=4 * T, align_bytes=64)
-        w_scales = shared.tile([P, N], U8, name="w_scales", offset=4 * T + 2 * N, align_bytes=64)
-        b_col = shared.tile([P, 1], F32, name="b_col", offset=4 * T + 3 * N, align_bytes=64)
+        w_codes = shared.tile([P, 2 * N], U8, name="w_codes", offset=SMALL_AT, align_bytes=64)
+        w_scales = shared.tile([P, N], U8, name="w_scales", offset=SMALL_AT + 2 * N, align_bytes=64)
+        b_col = shared.tile([P, 1], F32, name="b_col", offset=SMALL_AT + 3 * N, align_bytes=64)
         nc.sync.dma_start(out=w_codes[:].bitcast(I32), in_=w4_words[0].bitcast(I32))
         nc.sync.dma_start(out=b_col[:], in_=b.rearrange("(p o) -> p o", o=1))
         for q in range(4):
             nc.sync.dma_start(
                 out=w_scales[32 * q : 32 * q + 4, :].bitcast(I32), in_=w4_scales[0, 4 * q : 4 * q + 4, :].bitcast(I32)
             )
-        words2 = shared.tile([P, T], I32, name="words2", offset=0, align_bytes=64)
+        words2 = shared.tile([P, T], I32, name="words2", offset=PAIR1_AT, align_bytes=64)
         nc.sync.dma_start(out=words2[:], in_=tab2[1:2, :WORDS].bitcast(I32).rearrange("o (p t) -> (o p) t", p=P))
-        plane1 = keep.tile([P, S], U8, name="plane1", align_bytes=64)
+        got0 = keep.tile([P, S], U32, name="got0", align_bytes=64)
+        nc.vector.tensor_copy(got0[:], words0[:].bitcast(U32).indirect(list2[:]))
+        plane1 = shared.tile([P, S], U8, name="plane1", offset=PLANE1_AT, align_bytes=64)
         nc.vector.tensor_copy(plane1[:], win1[:].bitcast(U8).indirect(list1[:]))
-        planes = shared.tile([P, 4 * S], U8, name="planes", offset=WIN2_AT + LAP, align_bytes=64)
-        for q in (0, 2, 1, 3):
-            nc.sync.dma_start(
-                out=planes[32 * q : 32 * q + 4, :].bitcast(I32).rearrange("r (a c) -> r a c", a=4),
-                in_=got2[32 + 16 * q : 48 + 16 * q, :].bitcast(I32),
-            )
+        planes = shared.tile([P, 4 * S], U8, name="planes", offset=0, align_bytes=64)
 
-        words1 = shared.tile([P, T], I32, name="words_tab", offset=WIN2_AT + 2 * T - LAP, align_bytes=64)
+        def move_rows(m):
+            for q in (0, 2, 1, 3):
+                nc.sync.dma_start(
+                    out=planes[32 * q : 32 * q + 4, 2 * S * m : 2 * S * (m + 1)].bitcast(I32).rearrange("r (h c) -> r h c", h=2),
+                    in_=got2[32 + 16 * q + m : 48 + 16 * q : 2, :].bitcast(I32),
+                )
+
+        move_rows(0)
+        words1 = shared.tile([P, T], I32, name="words_tab", offset=TAB_AT, align_bytes=64)
         nc.sync.dma_start(out=words1[:], in_=tab[0:1, :WORDS].bitcast(I32).rearrange("o (p t) -> (o p) t", p=P))
+        move_rows(1)
 
         grouped = keep.tile([P, 4, N, 4], BF16, name="grouped", align_bytes=64)
         nc.scalar.copy(out=grouped[:], in_=raw[:].rearrange("p a i n -> p a n i"))
         u_codes = keep.tile([P, 4 * N], U32, name="u_codes", align_bytes=64)
         u_scales = keep.tile([P, 4 * N], U8, name="u_scales", align_bytes=64)
 
-        acc = [psum.tile([P, SLICE], F32, name=f"acc{s}") for s in range(3)]
+        spans = [(0, SLICE), (SLICE, SLICE)] + [(2 * SLICE + P * t, P) for t in range(4)]
+        acc = [psum.tile([P, width], F32, name=f"acc{g}", tag=f"acc{g}") for g, (first, width) in enumerate(spans)]
+        groups = [[0], [1], [2, 3, 4, 5]]
 
         def part(dst, src):
             nc.vector.tensor_copy(
@@ -100,33 +111,35 @@ def tile_list_tab48_tm_silu_kernel(tc, tab, w4_words, w4_scales, tab2, u, b, off
                 src[:].bitcast(U16).rearrange("p (j h) -> p h j", h=2),
             )
 
-        def pass2(a, s, codes, first):
-            plane = S * (2 * (a % 2) + a // 2) + SLICE * s
-            nc.tensor.matmul_mx(
-                out=acc[s][:],
-                lhsT=u_codes[:, N * a : N * (a + 1)].bitcast(FP8X4),
-                lhsT_scale=u_scales[:, N * a : N * (a + 1)],
-                rhs=codes[:, first : first + 2 * SLICE].bitcast(FP4X4),
-                rhs_scale=planes[:, plane : plane + SLICE],
-                start=(a == 0),
-                stop=False,
-            )
+        def pass2(a, s, codes, base):
+            for g in groups[s]:
+                first, width = spans[g]
+                at = base + 2 * (first - SLICE * s)
+                nc.tensor.matmul_mx(
+                    out=acc[g][:],
+                    lhsT=u_codes[:, N * a : N * (a + 1)].bitcast(FP8X4),
+                    lhsT_scale=u_scales[:, N * a : N * (a + 1)],
+                    rhs=codes[:, at : at + 2 * width].bitcast(FP4X4),
+                    rhs_scale=planes[:, S * a + first : S * a + first + width],
+                    start=(a == 0),
+                    stop=False,
+                )
 
         def pass1(s):
-            nc.tensor.matmul_mx(
-                out=acc[s][:],
-                lhsT=w_codes[:].bitcast(FP4X4),
-                lhsT_scale=w_scales[:],
-                rhs=codes1[:, SLICE * s : SLICE * (s + 1)].bitcast(FP8X4),
-                rhs_scale=plane1[:, SLICE * s : SLICE * (s + 1)],
-                start=False,
-                stop=True,
-            )
+            for g in groups[s]:
+                first, width = spans[g]
+                nc.tensor.matmul_mx(
+                    out=acc[g][:],
+                    lhsT=w_codes[:].bitcast(FP4X4),
+                    lhsT_scale=w_scales[:],
+                    rhs=codes1[:, first : first + width].bitcast(FP8X4),
+                    rhs_scale=plane1[:, first : first + width],
+                    start=False,
+                    stop=True,
+                )
 
-        got0 = keep.tile([P, S], U32, name="got0", align_bytes=64)
         parted0 = keep.tile([P, 4 * S], U8, name="parted0", align_bytes=64)
         codes1 = keep.tile([P, S], U32, name="codes1", align_bytes=64)
-        nc.vector.tensor_copy(got0[:], words0[:].bitcast(U32).indirect(list2[:]))
         part(parted0, got0)
         nc.vector.quantize_mx(
             out=u_codes[:].bitcast(FP8X4), scales=u_scales[:], in_=grouped[:].rearrange("p a n i -> p (a n i)")
@@ -135,21 +148,19 @@ def tile_list_tab48_tm_silu_kernel(tc, tab, w4_words, w4_scales, tab2, u, b, off
             for s in range(3):
                 pass2(a, s, parted0, a * 2 * S + 2 * SLICE * s)
 
-        def finish(s, pieces, copies, stores):
-            width = SLICE // pieces
-            tiles = width // P
-            res = keep.tile([P, 4, N], F32, name=f"res{s}")
-            for h in range(pieces):
-                act = keep.tile([P, width], F32, name=f"act{s}_{h}")
-                nc.scalar.activation(act[:], acc[s][:, width * h : width * (h + 1)], SILU, bias=b_col[:])
-                turned = psum.tile([P, tiles, N], F32, name=f"turned{s}_{h}", tag=f"turned{(s + h) % 5}")
-                for t in range(tiles):
-                    nc.tensor.transpose(turned[:, t, :], act[:, 128 * t : 128 * (t + 1)], ident[:])
-                copies[h % len(copies)](res[:, tiles * h : tiles * (h + 1), :], turned[:])
-            per = 4 // stores
-            for h in range(stores):
-                rows = out[SLICE * s + P * per * h : SLICE * s + P * per * (h + 1), :]
-                nc.sync.dma_start(out=rows.rearrange("(t p) n -> p t n", p=P), in_=res[:, per * h : per * (h + 1), :])
+        def finish(g, lo, tiles, copy_out, tag):
+            at = spans[g][0] // P + lo
+            act = keep.tile([P, tiles, P], F32, name=f"act{at}")
+            dealt = acc[g][:].rearrange("n (p t) -> n t p", p=P)
+            nc.scalar.activation(act[:], dealt[:, lo : lo + tiles, :], SILU, bias=b_col[:])
+            turned = psum.tile([P, tiles, N], F32, name=f"turned{at}", tag=tag)
+            for t in range(tiles):
+                nc.tensor.transpose(turned[:, t, :], act[:, t, :], ident[:])
+            copy_out(res[:, at : at + tiles, :], turned[:])
+
+        def store(first, res, order):
+            rows = out[first : first + P * res.shape[1], :]
+            nc.sync.dma_start(out=rows.rearrange(order, p=P), in_=res)
 
         for s in range(3):
             got = keep.tile([P, SLICE], U32, name=f"got1_{s}", align_bytes=64)
@@ -167,6 +178,13 @@ def tile_list_tab48_tm_silu_kernel(tc, tab, w4_words, w4_scales, tab2, u, b, off
                 words1[:].bitcast(U32).indirect(list1[:, SLICE // 16 * s : SLICE // 16 * (s + 1)]),
             )
             pass1(s)
-        finish(0, 1, [nc.vector.tensor_copy], 1)
-        finish(1, 1, [nc.vector.tensor_copy], 1)
-        finish(2, 4, [nc.scalar.copy, nc.vector.tensor_copy], 2)
+        res = keep.tile([P, S // P, N], F32, name="res")
+        finish(0, 0, 4, nc.vector.tensor_copy, "turned0")
+        store(0, res[:, 0:4, :], "(p t) n -> p t n")
+        finish(1, 0, 2, nc.vector.tensor_copy, "turned1")
+        finish(1, 2, 2, nc.vector.tensor_copy, "acc0")
+        store(SLICE, res[:, 4:8, :], "(p t) n -> p t n")
+        for t in range(4):
+            finish(2 + t, 0, 1, nc.scalar.copy if t == 2 else nc.vector.tensor_copy, f"acc{2 + t}")
+        store(2 * SLICE, res[:, 8:11, :], "(t p) n -> p t n")
+        store(2 * SLICE + 3 * P, res[:, 11:12, :], "(t p) n -> p t n")

@@ -20,11 +20,13 @@ P = 128
 WORDS = 512 * T
 SLICE = 512
 COLS = S // 16
-PLANE1_AT = 4 * S
-TAB_AT = 2 * T
-PAIR1_AT = TAB_AT + 4 * T
-SMALL_AT = PAIR1_AT + 4 * T
-WIN2_AT = SMALL_AT - 512
+EDGE = 512
+WIN2_AT = 4 * T - EDGE
+WIN1_AT = WIN2_AT + T
+W_SCALES_AT = WIN2_AT + EDGE
+PLANES_AT = WIN2_AT + 2 * EDGE
+W_AT = PLANES_AT + 4 * S
+TAB_AT = WIN1_AT + T - EDGE
 
 
 def tile_list_tab48_tm_silu_kernel(tc, tab, w4_words, w4_scales, tab2, u, b, offs, offs2, out):
@@ -38,8 +40,8 @@ def tile_list_tab48_tm_silu_kernel(tc, tab, w4_words, w4_scales, tab2, u, b, off
         list2 = lists.tile([P, COLS], U16, name="list2")
         list1 = lists.tile([P, COLS], U16, name="list1")
         win2 = shared.tile([P, T // 4], I32, name="win2", offset=WIN2_AT, align_bytes=64)
-        win1 = keep.tile([P, T // 4], I32, name="win1")
-        seed = keep.tile([P, 1], F32, name="seed")
+        win1 = shared.tile([P, T // 4], I32, name="win1", offset=WIN1_AT, align_bytes=64)
+        seed = keep.tile([P, 1], F32, name="seed", tag="words0")
         warm = keep.tile([P, 1], F32, name="warm", tag="raw")
         nc.gpsimd.memset(seed[:], 0.0)
         nc.scalar.activation(warm[:], seed[:], SILU)
@@ -56,33 +58,27 @@ def tile_list_tab48_tm_silu_kernel(tc, tab, w4_words, w4_scales, tab2, u, b, off
                 out=win2[32 + m : 96 : 2, :],
                 in_=tab2[m : m + 1, WORDS:].bitcast(I32).rearrange("o (h q c) -> (o q) h c", h=2, q=16),
             )
-        words0 = shared.tile([P, T], I32, name="words0", offset=0, align_bytes=64)
-        nc.sync.dma_start(out=words0[:], in_=tab2[0:1, :WORDS].bitcast(I32).rearrange("o (p t) -> (o p) t", p=P))
         nc.sync.dma_start(list1[:], offs)
         scales1 = tab[0:1, WORDS:].bitcast(I32).rearrange("o (q c) -> (o q) c", c=T // 4)
         for q in (0, 2, 1, 3):
             nc.sync.dma_start(out=win1[32 * q : 32 * q + 4, :], in_=scales1[4 * q : 4 * q + 4, :])
+        words0 = keep.tile([P, T], I32, name="words0", tag="words0")
+        nc.sync.dma_start(out=words0[:], in_=tab2[0:1, :WORDS].bitcast(I32).rearrange("o (p t) -> (o p) t", p=P))
         raw = keep.tile([P, 4, 4, N], F32, name="raw", tag="raw")
         nc.sync.dma_start(out=raw[:].rearrange("p a i n -> p a (i n)"), in_=u.rearrange("(a p i) n -> p a (i n)", a=4, i=4))
 
         got2 = keep.tile([P, S], U8, name="got2", align_bytes=64)
         nc.vector.tensor_copy(got2[:], win2[:].bitcast(U8).indirect(list2[:]))
-        w_codes = shared.tile([P, 2 * N], U8, name="w_codes", offset=SMALL_AT, align_bytes=64)
-        w_scales = shared.tile([P, N], U8, name="w_scales", offset=SMALL_AT + 2 * N, align_bytes=64)
-        b_col = shared.tile([P, 1], F32, name="b_col", offset=SMALL_AT + 3 * N, align_bytes=64)
-        nc.sync.dma_start(out=w_codes[:].bitcast(I32), in_=w4_words[0].bitcast(I32))
-        nc.sync.dma_start(out=b_col[:], in_=b.rearrange("(p o) -> p o", o=1))
+        w_scales = shared.tile([P, N], U8, name="w_scales", offset=W_SCALES_AT, align_bytes=64)
         for q in range(4):
             nc.sync.dma_start(
                 out=w_scales[32 * q : 32 * q + 4, :].bitcast(I32), in_=w4_scales[0, 4 * q : 4 * q + 4, :].bitcast(I32)
             )
-        words2 = shared.tile([P, T], I32, name="words2", offset=PAIR1_AT, align_bytes=64)
+        words2 = shared.tile([P, T], I32, name="words2", offset=0, align_bytes=64)
         nc.sync.dma_start(out=words2[:], in_=tab2[1:2, :WORDS].bitcast(I32).rearrange("o (p t) -> (o p) t", p=P))
-        got0 = keep.tile([P, S], U32, name="got0", align_bytes=64)
-        nc.vector.tensor_copy(got0[:], words0[:].bitcast(U32).indirect(list2[:]))
-        plane1 = shared.tile([P, S], U8, name="plane1", offset=PLANE1_AT, align_bytes=64)
+        plane1 = keep.tile([P, S], U8, name="plane1", align_bytes=64)
         nc.vector.tensor_copy(plane1[:], win1[:].bitcast(U8).indirect(list1[:]))
-        planes = shared.tile([P, 4 * S], U8, name="planes", offset=0, align_bytes=64)
+        planes = shared.tile([P, 4 * S], U8, name="planes", offset=PLANES_AT, align_bytes=64)
 
         def move_rows(m):
             for q in (0, 2, 1, 3):
@@ -91,10 +87,14 @@ def tile_list_tab48_tm_silu_kernel(tc, tab, w4_words, w4_scales, tab2, u, b, off
                     in_=got2[32 + 16 * q + m : 48 + 16 * q : 2, :].bitcast(I32),
                 )
 
-        move_rows(0)
+        move_rows(1)
         words1 = shared.tile([P, T], I32, name="words_tab", offset=TAB_AT, align_bytes=64)
         nc.sync.dma_start(out=words1[:], in_=tab[0:1, :WORDS].bitcast(I32).rearrange("o (p t) -> (o p) t", p=P))
-        move_rows(1)
+        move_rows(0)
+        w_codes = shared.tile([P, 2 * N], U8, name="w_codes", offset=W_AT, align_bytes=64)
+        b_col = shared.tile([P, 1], F32, name="b_col", offset=W_AT + 2 * N, align_bytes=64)
+        nc.sync.dma_start(out=w_codes[:].bitcast(I32), in_=w4_words[0].bitcast(I32))
+        nc.sync.dma_start(out=b_col[:], in_=b.rearrange("(p o) -> p o", o=1))
 
         grouped = keep.tile([P, 4, N, 4], BF16, name="grouped", align_bytes=64)
         nc.scalar.copy(out=grouped[:], in_=raw[:].rearrange("p a i n -> p a n i"))
@@ -121,7 +121,7 @@ def tile_list_tab48_tm_silu_kernel(tc, tab, w4_words, w4_scales, tab2, u, b, off
                     lhsT_scale=u_scales[:, N * a : N * (a + 1)],
                     rhs=codes[:, at : at + 2 * width].bitcast(FP4X4),
                     rhs_scale=planes[:, S * a + first : S * a + first + width],
-                    start=(a == 0),
+                    start=(a == 2),
                     stop=False,
                 )
 
@@ -138,15 +138,14 @@ def tile_list_tab48_tm_silu_kernel(tc, tab, w4_words, w4_scales, tab2, u, b, off
                     stop=True,
                 )
 
+        got0 = keep.tile([P, S], U32, name="got0", align_bytes=64)
+        nc.vector.tensor_copy(got0[:], words0[:].bitcast(U32).indirect(list2[:]))
         parted0 = keep.tile([P, 4 * S], U8, name="parted0", align_bytes=64)
         codes1 = keep.tile([P, S], U32, name="codes1", align_bytes=64)
         part(parted0, got0)
         nc.vector.quantize_mx(
             out=u_codes[:].bitcast(FP8X4), scales=u_scales[:], in_=grouped[:].rearrange("p a n i -> p (a n i)")
         )
-        for a in range(2):
-            for s in range(3):
-                pass2(a, s, parted0, a * 2 * S + 2 * SLICE * s)
 
         def finish(g, lo, tiles, copy_out, tag):
             at = spans[g][0] // P + lo
@@ -173,6 +172,8 @@ def tile_list_tab48_tm_silu_kernel(tc, tab, w4_words, w4_scales, tab2, u, b, off
                 pass2(2 + h, s, parted, h * 2 * SLICE)
 
         for s in range(3):
+            for a in range(2):
+                pass2(a, s, parted0, a * 2 * S + 2 * SLICE * s)
             nc.vector.tensor_copy(
                 codes1[:, SLICE * s : SLICE * (s + 1)],
                 words1[:].bitcast(U32).indirect(list1[:, SLICE // 16 * s : SLICE // 16 * (s + 1)]),
@@ -186,5 +187,5 @@ def tile_list_tab48_tm_silu_kernel(tc, tab, w4_words, w4_scales, tab2, u, b, off
         store(SLICE, res[:, 4:8, :], "(p t) n -> p t n")
         for t in range(4):
             finish(2 + t, 0, 1, nc.scalar.copy if t == 2 else nc.vector.tensor_copy, f"acc{2 + t}")
-        store(2 * SLICE, res[:, 8:11, :], "(t p) n -> p t n")
-        store(2 * SLICE + 3 * P, res[:, 11:12, :], "(t p) n -> p t n")
+        store(2 * SLICE, res[:, 8:10, :], "(t p) n -> p t n")
+        store(2 * SLICE + 2 * P, res[:, 10:12, :], "(t p) n -> p t n")

@@ -17,16 +17,20 @@ FP4X4 = mybir.dt.float4_e2m1fn_x4
 SILU = mybir.ActivationFunctionType.Silu
 
 P = 128
-WORDS = 512 * T
+WORD_BYTES = 512 * T
 SLICE = 512
-COLS = S // 16
+SLICES = S // SLICE
+LIST_COLS = S // 16
+QUADRANTS = (0, 2, 1, 3)
+
 EDGE = 512
-WIN2_AT = 4 * T - EDGE
-WIN1_AT = WIN2_AT + T
-W_SCALES_AT = WIN2_AT + EDGE
-PLANES_AT = WIN2_AT + 2 * EDGE
-W_AT = PLANES_AT + 4 * S
-TAB_AT = WIN1_AT + T - EDGE
+WINDOW2_AT = 4 * T - EDGE
+WINDOW1_AT = WINDOW2_AT + T
+W_SCALES_AT = WINDOW2_AT + EDGE
+PLANES2_AT = WINDOW2_AT + 2 * EDGE
+W_CODES_AT = PLANES2_AT + 4 * S
+BIAS_AT = W_CODES_AT + 2 * N
+TAB_WORDS_AT = WINDOW1_AT + T - EDGE
 
 
 def tile_list_tab48_tm_silu_kernel(tc, tab, w4_words, w4_scales, tab2, u, b, offs, offs2, out):
@@ -37,155 +41,167 @@ def tile_list_tab48_tm_silu_kernel(tc, tab, w4_words, w4_scales, tab2, u, b, off
         shared = ctx.enter_context(tc.tile_pool(name="shared", bufs=1))
         psum = ctx.enter_context(tc.psum_pool(name="psum", bufs=1))
 
-        list2 = lists.tile([P, COLS], U16, name="list2")
-        list1 = lists.tile([P, COLS], U16, name="list1")
-        win2 = shared.tile([P, T // 4], I32, name="win2", offset=WIN2_AT, align_bytes=64)
-        win1 = shared.tile([P, T // 4], I32, name="win1", offset=WIN1_AT, align_bytes=64)
-        seed = keep.tile([P, 1], F32, name="seed", tag="words0")
-        warm = keep.tile([P, 1], F32, name="warm", tag="raw")
+        def load_words(tile, row):
+            nc.sync.dma_start(out=tile[:], in_=row[:, :WORD_BYTES].bitcast(I32).rearrange("o (p t) -> (o p) t", p=P))
+
+        def gather(dst, window, offsets, first, count):
+            nc.vector.tensor_copy(dst, window.indirect(offsets[:, first // 16 : (first + count) // 16]))
+
+        def part(parted, pairs, first, count):
+            cols = slice(first, first + count)
+            nc.vector.tensor_copy(
+                parted[:].bitcast(U16).rearrange("p (h j) -> p h j", h=2)[:, :, cols],
+                pairs[:].bitcast(U16).rearrange("p (j h) -> p h j", h=2)[:, :, cols],
+            )
+
+        list2 = lists.tile([P, LIST_COLS], U16, name="list2")
+        list1 = lists.tile([P, LIST_COLS], U16, name="list1")
+        window2 = shared.tile([P, T // 4], I32, name="window2", offset=WINDOW2_AT, align_bytes=64)
+        window1 = shared.tile([P, T // 4], I32, name="window1", offset=WINDOW1_AT, align_bytes=64)
+
+        seed = keep.tile([P, 1], F32, name="seed", tag="pair0_words")
+        warm = keep.tile([P, 1], F32, name="warm", tag="u_rows")
         nc.gpsimd.memset(seed[:], 0.0)
         nc.scalar.activation(warm[:], seed[:], SILU)
 
-        nc.gpsimd.memset(win1[:], 0)
-        nc.vector.memset(win2[0:32, :], 0)
-        nc.vector.memset(win2[96:128, :], 0)
+        nc.gpsimd.memset(window1[:], 0)
+        nc.vector.memset(window2[0:32, :], 0)
+        nc.vector.memset(window2[96:128, :], 0)
         ident = keep.tile([P, P], F32, name="ident")
         make_identity(nc, ident[:])
 
         nc.sync.dma_start(list2[:], offs2)
         for m in range(2):
             nc.sync.dma_start(
-                out=win2[32 + m : 96 : 2, :],
-                in_=tab2[m : m + 1, WORDS:].bitcast(I32).rearrange("o (h q c) -> (o q) h c", h=2, q=16),
+                out=window2[32 + m : 96 : 2, :],
+                in_=tab2[m : m + 1, WORD_BYTES:].bitcast(I32).rearrange("o (h q c) -> (o q) h c", h=2, q=16),
             )
         nc.sync.dma_start(list1[:], offs)
-        scales1 = tab[0:1, WORDS:].bitcast(I32).rearrange("o (q c) -> (o q) c", c=T // 4)
-        for q in (0, 2, 1, 3):
-            nc.sync.dma_start(out=win1[32 * q : 32 * q + 4, :], in_=scales1[4 * q : 4 * q + 4, :])
-        words0 = keep.tile([P, T], I32, name="words0", tag="words0")
-        nc.sync.dma_start(out=words0[:], in_=tab2[0:1, :WORDS].bitcast(I32).rearrange("o (p t) -> (o p) t", p=P))
-        raw = keep.tile([P, 4, 4, N], F32, name="raw", tag="raw")
-        nc.sync.dma_start(out=raw[:].rearrange("p a i n -> p a (i n)"), in_=u.rearrange("(a p i) n -> p a (i n)", a=4, i=4))
+        tab_scale_rows = tab[0:1, WORD_BYTES:].bitcast(I32).rearrange("o (q c) -> (o q) c", c=T // 4)
+        for quad in QUADRANTS:
+            nc.sync.dma_start(out=window1[32 * quad : 32 * quad + 4, :], in_=tab_scale_rows[4 * quad : 4 * quad + 4, :])
+        pair0_words = keep.tile([P, T], I32, name="pair0_words", tag="pair0_words")
+        load_words(pair0_words, tab2[0:1])
+        u_rows = keep.tile([P, 4, 4, N], F32, name="u_rows", tag="u_rows")
+        nc.sync.dma_start(
+            out=u_rows[:].rearrange("p a i n -> p a (i n)"), in_=u.rearrange("(a p i) n -> p a (i n)", a=4, i=4)
+        )
 
-        got2 = keep.tile([P, S], U8, name="got2", align_bytes=64)
-        nc.vector.tensor_copy(got2[:], win2[:].bitcast(U8).indirect(list2[:]))
+        scales2 = keep.tile([P, S], U8, name="scales2", align_bytes=64)
+        gather(scales2[:], window2[:].bitcast(U8), list2, 0, S)
         w_scales = shared.tile([P, N], U8, name="w_scales", offset=W_SCALES_AT, align_bytes=64)
-        for q in range(4):
+        for quad in range(4):
             nc.sync.dma_start(
-                out=w_scales[32 * q : 32 * q + 4, :].bitcast(I32), in_=w4_scales[0, 4 * q : 4 * q + 4, :].bitcast(I32)
+                out=w_scales[32 * quad : 32 * quad + 4, :].bitcast(I32),
+                in_=w4_scales[0, 4 * quad : 4 * quad + 4, :].bitcast(I32),
             )
-        words2 = shared.tile([P, T], I32, name="words2", offset=0, align_bytes=64)
-        nc.sync.dma_start(out=words2[:], in_=tab2[1:2, :WORDS].bitcast(I32).rearrange("o (p t) -> (o p) t", p=P))
+        pair1_words = shared.tile([P, T], I32, name="pair1_words", offset=0, align_bytes=64)
+        load_words(pair1_words, tab2[1:2])
         plane1 = keep.tile([P, S], U8, name="plane1", align_bytes=64)
-        nc.vector.tensor_copy(plane1[:], win1[:].bitcast(U8).indirect(list1[:]))
-        planes = shared.tile([P, 4 * S], U8, name="planes", offset=PLANES_AT, align_bytes=64)
+        gather(plane1[:], window1[:].bitcast(U8), list1, 0, S)
 
-        def move_rows(m):
-            for q in (0, 2, 1, 3):
+        planes2 = shared.tile([P, 4 * S], U8, name="planes2", offset=PLANES2_AT, align_bytes=64)
+
+        def move_scale_rows(m):
+            for quad in QUADRANTS:
                 nc.sync.dma_start(
-                    out=planes[32 * q : 32 * q + 4, 2 * S * m : 2 * S * (m + 1)].bitcast(I32).rearrange("r (h c) -> r h c", h=2),
-                    in_=got2[32 + 16 * q + m : 48 + 16 * q : 2, :].bitcast(I32),
+                    out=planes2[32 * quad : 32 * quad + 4, 2 * S * m : 2 * S * (m + 1)]
+                    .bitcast(I32)
+                    .rearrange("r (h c) -> r h c", h=2),
+                    in_=scales2[32 + 16 * quad + m : 48 + 16 * quad : 2, :].bitcast(I32),
                 )
 
-        move_rows(1)
-        words1 = shared.tile([P, T], I32, name="words_tab", offset=TAB_AT, align_bytes=64)
-        nc.sync.dma_start(out=words1[:], in_=tab[0:1, :WORDS].bitcast(I32).rearrange("o (p t) -> (o p) t", p=P))
-        move_rows(0)
-        w_codes = shared.tile([P, 2 * N], U8, name="w_codes", offset=W_AT, align_bytes=64)
-        b_col = shared.tile([P, 1], F32, name="b_col", offset=W_AT + 2 * N, align_bytes=64)
+        move_scale_rows(1)
+        tab_words = shared.tile([P, T], I32, name="tab_words", offset=TAB_WORDS_AT, align_bytes=64)
+        load_words(tab_words, tab[0:1])
+        move_scale_rows(0)
+        w_codes = shared.tile([P, 2 * N], U8, name="w_codes", offset=W_CODES_AT, align_bytes=64)
+        bias = shared.tile([P, 1], F32, name="bias", offset=BIAS_AT, align_bytes=64)
         nc.sync.dma_start(out=w_codes[:].bitcast(I32), in_=w4_words[0].bitcast(I32))
-        nc.sync.dma_start(out=b_col[:], in_=b.rearrange("(p o) -> p o", o=1))
+        nc.sync.dma_start(out=bias[:], in_=b.rearrange("(p o) -> p o", o=1))
 
-        grouped = keep.tile([P, 4, N, 4], BF16, name="grouped", align_bytes=64)
-        nc.scalar.copy(out=grouped[:], in_=raw[:].rearrange("p a i n -> p a n i"))
+        u_grouped = keep.tile([P, 4, N, 4], BF16, name="u_grouped", align_bytes=64)
+        nc.scalar.copy(out=u_grouped[:], in_=u_rows[:].rearrange("p a i n -> p a n i"))
         u_codes = keep.tile([P, 4 * N], U32, name="u_codes", align_bytes=64)
         u_scales = keep.tile([P, 4 * N], U8, name="u_scales", align_bytes=64)
 
-        spans = [(0, SLICE), (SLICE, SLICE)] + [(2 * SLICE + P * t, P) for t in range(4)]
-        acc = [psum.tile([P, width], F32, name=f"acc{g}", tag=f"acc{g}") for g, (first, width) in enumerate(spans)]
-        groups = [[0], [1], [2, 3, 4, 5]]
+        sums = [(0, SLICE), (SLICE, SLICE)] + [(2 * SLICE + P * t, P) for t in range(4)]
+        sums_of_slice = [[0], [1], [2, 3, 4, 5]]
+        acc = [psum.tile([P, items], F32, name=f"acc{g}", tag=f"acc{g}") for g, (first, items) in enumerate(sums)]
 
-        def part(dst, src):
-            nc.vector.tensor_copy(
-                dst[:].bitcast(U16).rearrange("p (h j) -> p h j", h=2),
-                src[:].bitcast(U16).rearrange("p (j h) -> p h j", h=2),
-            )
-
-        def pass2(a, s, codes, base):
-            for g in groups[s]:
-                first, width = spans[g]
-                at = base + 2 * (first - SLICE * s)
+        def tab2_pass(a, s, parted, slice_at):
+            for g in sums_of_slice[s]:
+                first, items = sums[g]
+                at = slice_at + 2 * (first - SLICE * s)
                 nc.tensor.matmul_mx(
                     out=acc[g][:],
                     lhsT=u_codes[:, N * a : N * (a + 1)].bitcast(FP8X4),
                     lhsT_scale=u_scales[:, N * a : N * (a + 1)],
-                    rhs=codes[:, at : at + 2 * width].bitcast(FP4X4),
-                    rhs_scale=planes[:, S * a + first : S * a + first + width],
+                    rhs=parted[:, at : at + 2 * items].bitcast(FP4X4),
+                    rhs_scale=planes2[:, S * a + first : S * a + first + items],
                     start=(a == 2),
                     stop=False,
                 )
 
-        def pass1(s):
-            for g in groups[s]:
-                first, width = spans[g]
+        def tab_pass(s):
+            for g in sums_of_slice[s]:
+                first, items = sums[g]
                 nc.tensor.matmul_mx(
                     out=acc[g][:],
                     lhsT=w_codes[:].bitcast(FP4X4),
                     lhsT_scale=w_scales[:],
-                    rhs=codes1[:, first : first + width].bitcast(FP8X4),
-                    rhs_scale=plane1[:, first : first + width],
+                    rhs=tab_codes[:, first : first + items].bitcast(FP8X4),
+                    rhs_scale=plane1[:, first : first + items],
                     start=False,
                     stop=True,
                 )
 
-        got0 = keep.tile([P, S], U32, name="got0", align_bytes=64)
-        nc.vector.tensor_copy(got0[:], words0[:].bitcast(U32).indirect(list2[:]))
+        pairs0 = keep.tile([P, S], U32, name="pairs0", align_bytes=64)
+        for first in (0, S // 2):
+            gather(pairs0[:, first : first + S // 2], pair0_words[:].bitcast(U32), list2, first, S // 2)
         parted0 = keep.tile([P, 4 * S], U8, name="parted0", align_bytes=64)
-        codes1 = keep.tile([P, S], U32, name="codes1", align_bytes=64)
-        part(parted0, got0)
+        tab_codes = keep.tile([P, S], U32, name="tab_codes", align_bytes=64)
+        for first in (0, S // 2):
+            part(parted0, pairs0, first, S // 2)
         nc.vector.quantize_mx(
-            out=u_codes[:].bitcast(FP8X4), scales=u_scales[:], in_=grouped[:].rearrange("p a n i -> p (a n i)")
+            out=u_codes[:].bitcast(FP8X4), scales=u_scales[:], in_=u_grouped[:].rearrange("p a n i -> p (a n i)")
         )
 
-        def finish(g, lo, tiles, copy_out, tag):
-            at = spans[g][0] // P + lo
+        for s in range(SLICES):
+            pairs1 = keep.tile([P, SLICE], U32, name=f"pairs1_{s}", align_bytes=64)
+            parted1 = keep.tile([P, 4 * SLICE], U8, name=f"parted1_{s}", align_bytes=64)
+            gather(pairs1[:], pair1_words[:].bitcast(U32), list2, SLICE * s, SLICE)
+            part(parted1, pairs1, 0, SLICE)
+            for h in range(2):
+                tab2_pass(2 + h, s, parted1, 2 * SLICE * h)
+
+        for s in range(SLICES):
+            for h in range(2):
+                tab2_pass(h, s, parted0, 2 * S * h + 2 * SLICE * s)
+            gather(tab_codes[:, SLICE * s : SLICE * (s + 1)], tab_words[:].bitcast(U32), list1, SLICE * s, SLICE)
+            tab_pass(s)
+
+        staged = keep.tile([P, S // P, N], F32, name="staged")
+
+        def finish(g, lo, tiles, copy_out, bank):
+            at = sums[g][0] // P + lo
             act = keep.tile([P, tiles, P], F32, name=f"act{at}")
             dealt = acc[g][:].rearrange("n (p t) -> n t p", p=P)
-            nc.scalar.activation(act[:], dealt[:, lo : lo + tiles, :], SILU, bias=b_col[:])
-            turned = psum.tile([P, tiles, N], F32, name=f"turned{at}", tag=tag)
+            nc.scalar.activation(act[:], dealt[:, lo : lo + tiles, :], SILU, bias=bias[:])
+            turned = psum.tile([P, tiles, N], F32, name=f"turned{at}", tag=bank)
             for t in range(tiles):
                 nc.tensor.transpose(turned[:, t, :], act[:, t, :], ident[:])
-            copy_out(res[:, at : at + tiles, :], turned[:])
+            copy_out(staged[:, at : at + tiles, :], turned[:])
 
-        def store(first, res, order):
-            rows = out[first : first + P * res.shape[1], :]
-            nc.sync.dma_start(out=rows.rearrange(order, p=P), in_=res)
+        for g, banks in enumerate((("spare0", "spare1"), ("acc0", "acc1"))):
+            rows = out[SLICE * g : SLICE * (g + 1), :].rearrange("(p t) n -> p t n", p=P)
+            for half in range(2):
+                lo = 2 * half
+                finish(g, lo, 2, nc.scalar.copy if (g, half) == (1, 1) else nc.vector.tensor_copy, banks[half])
+                nc.sync.dma_start(out=rows[:, lo : lo + 2, :], in_=staged[:, 4 * g + lo : 4 * g + lo + 2, :])
 
-        for s in range(3):
-            got = keep.tile([P, SLICE], U32, name=f"got1_{s}", align_bytes=64)
-            parted = keep.tile([P, 4 * SLICE], U8, name=f"parted1_{s}", align_bytes=64)
-            nc.vector.tensor_copy(
-                got[:], words2[:].bitcast(U32).indirect(list2[:, SLICE // 16 * s : SLICE // 16 * (s + 1)])
-            )
-            part(parted, got)
-            for h in range(2):
-                pass2(2 + h, s, parted, h * 2 * SLICE)
-
-        for s in range(3):
-            for a in range(2):
-                pass2(a, s, parted0, a * 2 * S + 2 * SLICE * s)
-            nc.vector.tensor_copy(
-                codes1[:, SLICE * s : SLICE * (s + 1)],
-                words1[:].bitcast(U32).indirect(list1[:, SLICE // 16 * s : SLICE // 16 * (s + 1)]),
-            )
-            pass1(s)
-        res = keep.tile([P, S // P, N], F32, name="res")
-        finish(0, 0, 4, nc.vector.tensor_copy, "turned0")
-        store(0, res[:, 0:4, :], "(p t) n -> p t n")
-        finish(1, 0, 2, nc.vector.tensor_copy, "turned1")
-        finish(1, 2, 2, nc.vector.tensor_copy, "acc0")
-        store(SLICE, res[:, 4:8, :], "(p t) n -> p t n")
         for t in range(4):
-            finish(2 + t, 0, 1, nc.scalar.copy if t == 2 else nc.vector.tensor_copy, f"acc{2 + t}")
-        store(2 * SLICE, res[:, 8:10, :], "(t p) n -> p t n")
-        store(2 * SLICE + 2 * P, res[:, 10:12, :], "(t p) n -> p t n")
+            finish(2 + t, 0, 1, nc.vector.tensor_copy if t < 2 else nc.scalar.copy, f"acc{2 + t}")
+        for at in (8, 10):
+            rows = out[P * at : P * (at + 2), :].rearrange("(t p) n -> p t n", p=P)
+            nc.sync.dma_start(out=rows, in_=staged[:, at : at + 2, :])

@@ -27,9 +27,10 @@ EDGE = 512
 WINDOW2_AT = 4 * T - EDGE
 WINDOW1_AT = WINDOW2_AT + T
 W_SCALES_AT = WINDOW2_AT + EDGE
+BIAS_AT = W_SCALES_AT + N
 PLANES2_AT = WINDOW2_AT + 2 * EDGE
+EARLY = 2 * SLICE
 W_CODES_AT = PLANES2_AT + 4 * S
-BIAS_AT = W_CODES_AT + 2 * N
 TAB_WORDS_AT = WINDOW1_AT + T - EDGE
 
 
@@ -95,66 +96,81 @@ def tile_list_tab48_tm_silu_kernel(tc, tab, w4_words, w4_scales, tab2, u, b, off
                 out=w_scales[32 * quad : 32 * quad + 4, :].bitcast(I32),
                 in_=w4_scales[0, 4 * quad : 4 * quad + 4, :].bitcast(I32),
             )
+        bias = shared.tile([P, 1], F32, name="bias", offset=BIAS_AT, align_bytes=64)
+        nc.sync.dma_start(out=bias[:], in_=b.rearrange("(p o) -> p o", o=1))
         pair1_words = shared.tile([P, T], I32, name="pair1_words", offset=0, align_bytes=64)
         load_words(pair1_words, tab2[1:2])
         plane1 = keep.tile([P, S], U8, name="plane1", align_bytes=64)
         gather(plane1[:], window1[:].bitcast(U8), list1, 0, S)
 
-        planes2 = shared.tile([P, 4 * S], U8, name="planes2", offset=PLANES2_AT, align_bytes=64)
+        early = shared.tile([P, 4 * EARLY], U8, name="early", offset=PLANES2_AT, align_bytes=64)
+        late = shared.tile([P, 4 * SLICE], U8, name="late", offset=PLANES2_AT + 4 * EARLY, align_bytes=64)
 
-        def move_scale_rows(m):
+        def move_scale_rows(planes, first, count):
             for quad in QUADRANTS:
                 nc.sync.dma_start(
-                    out=planes2[32 * quad : 32 * quad + 4, 2 * S * m : 2 * S * (m + 1)]
-                    .bitcast(I32)
-                    .rearrange("r (h c) -> r h c", h=2),
-                    in_=scales2[32 + 16 * quad + m : 48 + 16 * quad : 2, :].bitcast(I32),
+                    out=planes[32 * quad : 32 * quad + 4, :].bitcast(I32).rearrange("r (a c) -> r a c", a=4),
+                    in_=scales2[32 + 16 * quad : 48 + 16 * quad, first : first + count].bitcast(I32),
                 )
 
-        move_scale_rows(1)
+        def plane_of(a, first, count):
+            at = 2 * (a % 2) + a // 2
+            if first < EARLY:
+                return early[:, EARLY * at + first : EARLY * at + first + count]
+            return late[:, SLICE * at + first - EARLY : SLICE * at + first - EARLY + count]
+
+        move_scale_rows(early, 0, EARLY)
         tab_words = shared.tile([P, T], I32, name="tab_words", offset=TAB_WORDS_AT, align_bytes=64)
         load_words(tab_words, tab[0:1])
-        move_scale_rows(0)
+        move_scale_rows(late, EARLY, SLICE)
         w_codes = shared.tile([P, 2 * N], U8, name="w_codes", offset=W_CODES_AT, align_bytes=64)
-        bias = shared.tile([P, 1], F32, name="bias", offset=BIAS_AT, align_bytes=64)
         nc.sync.dma_start(out=w_codes[:].bitcast(I32), in_=w4_words[0].bitcast(I32))
-        nc.sync.dma_start(out=bias[:], in_=b.rearrange("(p o) -> p o", o=1))
+
+        spread = psum.tile([P, N], F32, name="spread", tag="spare1")
+        nc.tensor.transpose(spread[:], bias[:].to_broadcast([P, P]), ident[:])
+        bias_rows = keep.tile([P, N], F32, name="bias_rows")
+        nc.scalar.copy(bias_rows[:], spread[:])
 
         u_grouped = keep.tile([P, 4, N, 4], BF16, name="u_grouped", align_bytes=64)
         nc.scalar.copy(out=u_grouped[:], in_=u_rows[:].rearrange("p a i n -> p a n i"))
         u_codes = keep.tile([P, 4 * N], U32, name="u_codes", align_bytes=64)
         u_scales = keep.tile([P, 4 * N], U8, name="u_scales", align_bytes=64)
 
-        sums = [(0, SLICE), (SLICE, SLICE)] + [(2 * SLICE + P * t, P) for t in range(4)]
-        sums_of_slice = [[0], [1], [2, 3, 4, 5]]
-        acc = [psum.tile([P, items], F32, name=f"acc{g}", tag=f"acc{g}") for g, (first, items) in enumerate(sums)]
+        acc = [psum.tile([P, SLICE], F32, name=f"acc{g}", tag=f"acc{g}") for g in range(2)]
+        last = [psum.tile([P, N], F32, name=f"last{t}", tag=f"last{t}") for t in range(4)]
 
-        def tab2_pass(a, s, parted, slice_at):
-            for g in sums_of_slice[s]:
-                first, items = sums[g]
-                at = slice_at + 2 * (first - SLICE * s)
+        def multiply(s, codes, width, scales, w, w_scale, fmt, w_fmt, start, stop):
+            if s < 2:
                 nc.tensor.matmul_mx(
-                    out=acc[g][:],
-                    lhsT=u_codes[:, N * a : N * (a + 1)].bitcast(FP8X4),
-                    lhsT_scale=u_scales[:, N * a : N * (a + 1)],
-                    rhs=parted[:, at : at + 2 * items].bitcast(FP4X4),
-                    rhs_scale=planes2[:, S * a + first : S * a + first + items],
-                    start=(a == 2),
-                    stop=False,
+                    out=acc[s][:], lhsT=w.bitcast(w_fmt), lhsT_scale=w_scale, rhs=codes.bitcast(fmt), rhs_scale=scales,
+                    start=start, stop=stop,
                 )
+                return
+            for t in range(4):
+                nc.tensor.matmul_mx(
+                    out=last[t][:],
+                    lhsT=codes[:, width * P * t : width * P * (t + 1)].bitcast(fmt),
+                    lhsT_scale=scales[:, P * t : P * (t + 1)],
+                    rhs=w.bitcast(w_fmt),
+                    rhs_scale=w_scale,
+                    start=start,
+                    stop=stop,
+                )
+
+        def tab2_pass(a, s):
+            if a < 2:
+                codes = parted0[:, 2 * (S * a + SLICE * s) : 2 * (S * a + SLICE * (s + 1))]
+            else:
+                codes = parted1[s][:, 2 * SLICE * (a - 2) : 2 * SLICE * (a - 1)]
+            cols = slice(N * a, N * (a + 1))
+            multiply(s, codes, 2, plane_of(a, SLICE * s, SLICE), u_codes[:, cols], u_scales[:, cols], FP4X4, FP8X4, a == 0, False)
 
         def tab_pass(s):
-            for g in sums_of_slice[s]:
-                first, items = sums[g]
-                nc.tensor.matmul_mx(
-                    out=acc[g][:],
-                    lhsT=w_codes[:].bitcast(FP4X4),
-                    lhsT_scale=w_scales[:],
-                    rhs=tab_codes[:, first : first + items].bitcast(FP8X4),
-                    rhs_scale=plane1[:, first : first + items],
-                    start=False,
-                    stop=True,
-                )
+            cols = slice(SLICE * s, SLICE * (s + 1))
+            multiply(s, tab_codes[:, cols], 1, plane1[:, cols], w_codes[:], w_scales[:], FP8X4, FP4X4, False, True)
+
+        def tab_gather(s):
+            gather(tab_codes[:, SLICE * s : SLICE * (s + 1)], tab_words[:].bitcast(U32), list1, SLICE * s, SLICE)
 
         pairs0 = keep.tile([P, S], U32, name="pairs0", align_bytes=64)
         for first in (0, S // 2):
@@ -166,42 +182,53 @@ def tile_list_tab48_tm_silu_kernel(tc, tab, w4_words, w4_scales, tab2, u, b, off
         nc.vector.quantize_mx(
             out=u_codes[:].bitcast(FP8X4), scales=u_scales[:], in_=u_grouped[:].rearrange("p a n i -> p (a n i)")
         )
+        for s in range(2):
+            for a in range(2):
+                tab2_pass(a, s)
 
+        parted1 = [keep.tile([P, 4 * SLICE], U8, name=f"parted1_{s}", align_bytes=64) for s in range(SLICES)]
         for s in range(SLICES):
             pairs1 = keep.tile([P, SLICE], U32, name=f"pairs1_{s}", align_bytes=64)
-            parted1 = keep.tile([P, 4 * SLICE], U8, name=f"parted1_{s}", align_bytes=64)
             gather(pairs1[:], pair1_words[:].bitcast(U32), list2, SLICE * s, SLICE)
-            part(parted1, pairs1, 0, SLICE)
-            for h in range(2):
-                tab2_pass(2 + h, s, parted1, 2 * SLICE * h)
+            part(parted1[s], pairs1, 0, SLICE)
+            if s < 2:
+                for a in (2, 3):
+                    tab2_pass(a, s)
 
         for s in range(SLICES):
-            for h in range(2):
-                tab2_pass(h, s, parted0, 2 * S * h + 2 * SLICE * s)
-            gather(tab_codes[:, SLICE * s : SLICE * (s + 1)], tab_words[:].bitcast(U32), list1, SLICE * s, SLICE)
+            tab_gather(s)
+        for s in range(2):
+            for a in (2 * s, 2 * s + 1):
+                tab2_pass(a, 2)
             tab_pass(s)
 
         staged = keep.tile([P, S // P, N], F32, name="staged")
 
-        def finish(g, lo, tiles, copy_out, bank):
-            at = sums[g][0] // P + lo
-            act = keep.tile([P, tiles, P], F32, name=f"act{at}")
+        def finish(g, lo, copy_out, bank):
+            at = 4 * g + lo
+            act = keep.tile([P, 2, P], F32, name=f"act{at}")
             dealt = acc[g][:].rearrange("n (p t) -> n t p", p=P)
-            nc.scalar.activation(act[:], dealt[:, lo : lo + tiles, :], SILU, bias=bias[:])
-            turned = psum.tile([P, tiles, N], F32, name=f"turned{at}", tag=bank)
-            for t in range(tiles):
+            nc.scalar.activation(act[:], dealt[:, lo : lo + 2, :], SILU, bias=bias[:])
+            turned = psum.tile([P, 2, N], F32, name=f"turned{at}", tag=bank)
+            for t in range(2):
                 nc.tensor.transpose(turned[:, t, :], act[:, t, :], ident[:])
-            copy_out(staged[:, at : at + tiles, :], turned[:])
+            return lambda: copy_out(staged[:, at : at + 2, :], turned[:])
 
+        copies = []
         for g, banks in enumerate((("spare0", "spare1"), ("acc0", "acc1"))):
-            rows = out[SLICE * g : SLICE * (g + 1), :].rearrange("(p t) n -> p t n", p=P)
             for half in range(2):
-                lo = 2 * half
-                finish(g, lo, 2, nc.scalar.copy if (g, half) == (1, 1) else nc.vector.tensor_copy, banks[half])
-                nc.sync.dma_start(out=rows[:, lo : lo + 2, :], in_=staged[:, 4 * g + lo : 4 * g + lo + 2, :])
+                copies.append(finish(g, 2 * half, nc.scalar.copy if g == 0 else nc.vector.tensor_copy, banks[half]))
+        for c, copy in enumerate(copies):
+            g, lo = c // 2, 2 * (c % 2)
+            copy()
+            rows = out[SLICE * g : SLICE * (g + 1), :].rearrange("(p t) n -> p t n", p=P)
+            nc.sync.dma_start(out=rows[:, lo : lo + 2, :], in_=staged[:, 4 * g + lo : 4 * g + lo + 2, :])
 
+        tab_pass(2)
         for t in range(4):
-            finish(2 + t, 0, 1, nc.vector.tensor_copy if t < 2 else nc.scalar.copy, f"acc{2 + t}")
+            shifted = keep.tile([P, N], F32, name=f"shifted{t}")
+            nc.vector.tensor_tensor(shifted[:], last[t][:], bias_rows[:], mybir.AluOpType.add)
+            nc.scalar.activation(staged[:, 8 + t, :], shifted[:], SILU)
         for at in (8, 10):
             rows = out[P * at : P * (at + 2), :].rearrange("(t p) n -> p t n", p=P)
             nc.sync.dma_start(out=rows, in_=staged[:, at : at + 2, :])

@@ -65,7 +65,7 @@ def tile_list_tab48_tm_silu_kernel(tc, tab, w4_words, w4_scales, tab2, u, b, off
         nc.gpsimd.memset(seed[:], 0.0)
         nc.scalar.activation(warm[:], seed[:], SILU)
 
-        nc.gpsimd.memset(window1[:], 0)
+        nc.vector.memset(window1[:], 0)
         nc.vector.memset(window2[0:32, :], 0)
         nc.vector.memset(window2[96:128, :], 0)
         ident = keep.tile([P, P], F32, name="ident")

@@ -69,7 +69,8 @@ def tile_list_tab48_tm_silu_kernel(tc, tab, w4_words, w4_scales, tab2, u, b, off
         nc.vector.memset(window2[0:32, :], 0)
         nc.vector.memset(window2[96:128, :], 0)
         ident = keep.tile([P, P], F32, name="ident")
-        make_identity(nc, ident[:])
+        nc.vector.memset(ident[:], 0.0)
+        make_identity(nc, ident[:], nomemset=True)
 
         nc.sync.dma_start(list2[:], offs2)
         for m in range(2):

@@ -188,7 +188,7 @@ def tile_list_tab48_tm_silu_kernel(tc, tab, w4_words, w4_scales, tab2, u, b, off
                 tab2_pass(a, s)
 
         parted1 = [keep.tile([P, 4 * SLICE], U8, name=f"parted1_{s}", align_bytes=64) for s in range(SLICES)]
-        for s in range(SLICES):
+        for s in (2, 0, 1):
             pairs1 = keep.tile([P, SLICE], U32, name=f"pairs1_{s}", align_bytes=64)
             gather(pairs1[:], pair1_words[:].bitcast(U32), list2, SLICE * s, SLICE)
             part(parted1[s], pairs1, 0, SLICE)
@@ -198,38 +198,51 @@ def tile_list_tab48_tm_silu_kernel(tc, tab, w4_words, w4_scales, tab2, u, b, off
 
         for s in range(SLICES):
             tab_gather(s)
-        for s in range(2):
-            for a in (2 * s, 2 * s + 1):
-                tab2_pass(a, 2)
-            tab_pass(s)
-
         staged = keep.tile([P, S // P, N], F32, name="staged")
 
-        def finish(g, lo, copy_out, bank):
-            at = 4 * g + lo
-            act = keep.tile([P, 2, P], F32, name=f"act{at}")
+        acts = {}
+
+        def activate(g, half):
+            act = keep.tile([P, 2, P], F32, name=f"act{g}{half}")
             dealt = acc[g][:].rearrange("n (p t) -> n t p", p=P)
-            nc.scalar.activation(act[:], dealt[:, lo : lo + 2, :], SILU, bias=bias[:])
-            turned = psum.tile([P, 2, N], F32, name=f"turned{at}", tag=bank)
+            nc.scalar.activation(act[:], dealt[:, 2 * half : 2 * half + 2, :], SILU, bias=bias[:])
+            acts[g, half] = act
+
+        def turn(g, half, bank):
+            turned = psum.tile([P, 2, N], F32, name=f"turned{g}{half}", tag=bank)
             for t in range(2):
-                nc.tensor.transpose(turned[:, t, :], act[:, t, :], ident[:])
-            return lambda: copy_out(staged[:, at : at + 2, :], turned[:])
+                nc.tensor.transpose(turned[:, t, :], acts[g, half][:, t, :], ident[:])
+            return turned
 
-        copies = []
-        for g, banks in enumerate((("spare0", "spare1"), ("acc0", "acc1"))):
-            for half in range(2):
-                copies.append(finish(g, 2 * half, nc.scalar.copy if g == 0 else nc.vector.tensor_copy, banks[half]))
-        for c, copy in enumerate(copies):
-            g, lo = c // 2, 2 * (c % 2)
-            copy()
+        def leave(g, half, turned, copy_out):
+            at = 4 * g + 2 * half
+            copy_out(staged[:, at : at + 2, :], turned[:])
             rows = out[SLICE * g : SLICE * (g + 1), :].rearrange("(p t) n -> p t n", p=P)
-            nc.sync.dma_start(out=rows[:, lo : lo + 2, :], in_=staged[:, 4 * g + lo : 4 * g + lo + 2, :])
+            nc.sync.dma_start(out=rows[:, 2 * half : 2 * half + 2, :], in_=staged[:, at : at + 2, :])
 
+        tab2_pass(0, 2)
+        tab_pass(0)
+        tab2_pass(1, 2)
+        tab2_pass(2, 2)
+        tab_pass(1)
+        for g in range(2):
+            for half in range(2):
+                activate(g, half)
+        turned0 = [turn(0, 0, "spare0"), turn(0, 1, "spare1")]
+        tab2_pass(3, 2)
+        turned1 = [turn(1, 0, "acc0")]
         tab_pass(2)
+        turned1.append(turn(1, 1, "acc1"))
+        leave(0, 0, turned0[0], nc.vector.tensor_copy)
+        leave(0, 1, turned0[1], nc.scalar.copy)
         for t in range(4):
             shifted = keep.tile([P, N], F32, name=f"shifted{t}")
             nc.vector.tensor_tensor(shifted[:], last[t][:], bias_rows[:], mybir.AluOpType.add)
+            if t == 0:
+                leave(1, 0, turned1[0], nc.scalar.copy)
             nc.scalar.activation(staged[:, 8 + t, :], shifted[:], SILU)
-        for at in (8, 10):
-            rows = out[P * at : P * (at + 2), :].rearrange("(t p) n -> p t n", p=P)
-            nc.sync.dma_start(out=rows, in_=staged[:, at : at + 2, :])
+            if t % 2 == 1:
+                at = 7 + t
+                rows = out[P * at : P * (at + 2), :].rearrange("(t p) n -> p t n", p=P)
+                nc.sync.dma_start(out=rows, in_=staged[:, at : at + 2, :])
+        leave(1, 1, turned1[1], nc.vector.tensor_copy)

@@ -26,11 +26,11 @@ QUADRANTS = (0, 2, 1, 3)
 EDGE = 512
 WINDOW2_AT = 4 * T - EDGE
 WINDOW1_AT = WINDOW2_AT + T
-W_SCALES_AT = WINDOW2_AT + EDGE
-BIAS_AT = W_SCALES_AT + N
 PLANES2_AT = WINDOW2_AT + 2 * EDGE
 EARLY = 2 * SLICE
 W_CODES_AT = PLANES2_AT + 4 * S
+W_SCALES_AT = W_CODES_AT + 2 * N
+BIAS_AT = W_SCALES_AT + N
 TAB_WORDS_AT = WINDOW1_AT + T - EDGE
 
 
@@ -91,14 +91,6 @@ def tile_list_tab48_tm_silu_kernel(tc, tab, w4_words, w4_scales, tab2, u, b, off
 
         scales2 = keep.tile([P, S], U8, name="scales2", align_bytes=64)
         gather(scales2[:], window2[:].bitcast(U8), list2, 0, S)
-        w_scales = shared.tile([P, N], U8, name="w_scales", offset=W_SCALES_AT, align_bytes=64)
-        for quad in range(4):
-            nc.sync.dma_start(
-                out=w_scales[32 * quad : 32 * quad + 4, :].bitcast(I32),
-                in_=w4_scales[0, 4 * quad : 4 * quad + 4, :].bitcast(I32),
-            )
-        bias = shared.tile([P, 1], F32, name="bias", offset=BIAS_AT, align_bytes=64)
-        nc.sync.dma_start(out=bias[:], in_=b.rearrange("(p o) -> p o", o=1))
         pair1_words = shared.tile([P, T], I32, name="pair1_words", offset=0, align_bytes=64)
         load_words(pair1_words, tab2[1:2])
         plane1 = keep.tile([P, S], U8, name="plane1", align_bytes=64)
@@ -121,11 +113,24 @@ def tile_list_tab48_tm_silu_kernel(tc, tab, w4_words, w4_scales, tab2, u, b, off
             return late[:, SLICE * at + first - EARLY : SLICE * at + first - EARLY + count]
 
         move_scale_rows(early, 0, EARLY)
-        tab_words = shared.tile([P, T], I32, name="tab_words", offset=TAB_WORDS_AT, align_bytes=64)
-        load_words(tab_words, tab[0:1])
-        move_scale_rows(late, EARLY, SLICE)
         w_codes = shared.tile([P, 2 * N], U8, name="w_codes", offset=W_CODES_AT, align_bytes=64)
         nc.sync.dma_start(out=w_codes[:].bitcast(I32), in_=w4_words[0].bitcast(I32))
+        bias = shared.tile([P, 1], F32, name="bias", offset=BIAS_AT, align_bytes=64)
+        nc.sync.dma_start(out=bias[:], in_=b.rearrange("(p o) -> p o", o=1))
+        tab_words = shared.tile([P, T], I32, name="tab_words", offset=TAB_WORDS_AT, align_bytes=64)
+        load_words(tab_words, tab[0:1])
+        w_scales = shared.tile([P, N], U8, name="w_scales", offset=W_SCALES_AT, align_bytes=64)
+
+        def load_w_scales(quads):
+            for quad in quads:
+                nc.sync.dma_start(
+                    out=w_scales[32 * quad : 32 * quad + 4, :].bitcast(I32),
+                    in_=w4_scales[0, 4 * quad : 4 * quad + 4, :].bitcast(I32),
+                )
+
+        load_w_scales(QUADRANTS[:3])
+        move_scale_rows(late, EARLY, SLICE)
+        load_w_scales(QUADRANTS[3:])
 
         spread = psum.tile([P, N], F32, name="spread", tag="spare1")
         nc.tensor.transpose(spread[:], bias[:].to_broadcast([P, P]), ident[:])
@@ -168,16 +173,17 @@ def tile_list_tab48_tm_silu_kernel(tc, tab, w4_words, w4_scales, tab2, u, b, off
 
         def tab_pass(s):
             cols = slice(SLICE * s, SLICE * (s + 1))
-            multiply(s, tab_codes[:, cols], 1, plane1[:, cols], w_codes[:], w_scales[:], FP8X4, FP4X4, False, True)
+            multiply(s, tab_codes[s][:], 1, plane1[:, cols], w_codes[:], w_scales[:], FP8X4, FP4X4, False, True)
 
         def tab_gather(s):
-            gather(tab_codes[:, SLICE * s : SLICE * (s + 1)], tab_words[:].bitcast(U32), list1, SLICE * s, SLICE)
+            tab_codes[s] = keep.tile([P, SLICE], U32, name=f"tab_codes{s}", tag=f"tab_codes{s % 2}", align_bytes=64)
+            gather(tab_codes[s][:], tab_words[:].bitcast(U32), list1, SLICE * s, SLICE)
 
         pairs0 = keep.tile([P, S], U32, name="pairs0", align_bytes=64)
         for first in (0, S // 2):
             gather(pairs0[:, first : first + S // 2], pair0_words[:].bitcast(U32), list2, first, S // 2)
         parted0 = keep.tile([P, 4 * S], U8, name="parted0", align_bytes=64)
-        tab_codes = keep.tile([P, S], U32, name="tab_codes", align_bytes=64)
+        tab_codes = {}
         for first in (0, S // 2):
             part(parted0, pairs0, first, S // 2)
         nc.vector.quantize_mx(
@@ -196,7 +202,7 @@ def tile_list_tab48_tm_silu_kernel(tc, tab, w4_words, w4_scales, tab2, u, b, off
                 for a in (2, 3):
                     tab2_pass(a, s)
 
-        for s in range(SLICES):
+        for s in range(2):
             tab_gather(s)
         staged = keep.tile([P, S // P, N], F32, name="staged")
 
@@ -205,7 +211,10 @@ def tile_list_tab48_tm_silu_kernel(tc, tab, w4_words, w4_scales, tab2, u, b, off
         def activate(g, half):
             act = keep.tile([P, 2, P], F32, name=f"act{g}{half}")
             dealt = acc[g][:].rearrange("n (p t) -> n t p", p=P)
-            nc.scalar.activation(act[:], dealt[:, 2 * half : 2 * half + 2, :], SILU, bias=bias[:])
+            step = 1 if (g, half) == (0, 0) else 2
+            for t in range(0, 2, step):
+                at = 2 * half + t
+                nc.scalar.activation(act[:, t : t + step, :], dealt[:, at : at + step, :], SILU, bias=bias[:])
             acts[g, half] = act
 
         def turn(g, half, bank):
@@ -222,6 +231,7 @@ def tile_list_tab48_tm_silu_kernel(tc, tab, w4_words, w4_scales, tab2, u, b, off
 
         tab2_pass(0, 2)
         tab_pass(0)
+        tab_gather(2)
         tab2_pass(1, 2)
         tab2_pass(2, 2)
         tab_pass(1)

@@ -176,7 +176,7 @@ def tile_list_tab48_tm_silu_kernel(tc, tab, w4_words, w4_scales, tab2, u, b, off
             multiply(s, tab_codes[s][:], 1, plane1[:, cols], w_codes[:], w_scales[:], FP8X4, FP4X4, False, True)
 
         def tab_gather(s):
-            tab_codes[s] = keep.tile([P, SLICE], U32, name=f"tab_codes{s}", tag=f"tab_codes{s % 2}", align_bytes=64)
+            tab_codes[s] = keep.tile([P, SLICE], U32, name=f"tab_codes{s}", align_bytes=64)
             gather(tab_codes[s][:], tab_words[:].bitcast(U32), list1, SLICE * s, SLICE)
 
         pairs0 = keep.tile([P, S], U32, name="pairs0", align_bytes=64)
@@ -194,13 +194,18 @@ def tile_list_tab48_tm_silu_kernel(tc, tab, w4_words, w4_scales, tab2, u, b, off
                 tab2_pass(a, s)
 
         parted1 = [keep.tile([P, 4 * SLICE], U8, name=f"parted1_{s}", align_bytes=64) for s in range(SLICES)]
-        for s in (2, 0, 1):
-            pairs1 = keep.tile([P, SLICE], U32, name=f"pairs1_{s}", align_bytes=64)
-            gather(pairs1[:], pair1_words[:].bitcast(U32), list2, SLICE * s, SLICE)
-            part(parted1[s], pairs1, 0, SLICE)
-            if s < 2:
-                for a in (2, 3):
-                    tab2_pass(a, s)
+        pairs1 = [keep.tile([P, SLICE], U32, name=f"pairs1_{s}", align_bytes=64) for s in range(SLICES)]
+        order = (0, 2, 1)
+        for step in range(SLICES + 1):
+            if step < SLICES:
+                s = order[step]
+                gather(pairs1[s][:], pair1_words[:].bitcast(U32), list2, SLICE * s, SLICE)
+            if step > 0:
+                s = order[step - 1]
+                part(parted1[s], pairs1[s], 0, SLICE)
+                if s < 2:
+                    for a in (2, 3):
+                        tab2_pass(a, s)
 
         for s in range(2):
             tab_gather(s)
@@ -211,10 +216,7 @@ def tile_list_tab48_tm_silu_kernel(tc, tab, w4_words, w4_scales, tab2, u, b, off
         def activate(g, half):
             act = keep.tile([P, 2, P], F32, name=f"act{g}{half}")
             dealt = acc[g][:].rearrange("n (p t) -> n t p", p=P)
-            step = 1 if (g, half) == (0, 0) else 2
-            for t in range(0, 2, step):
-                at = 2 * half + t
-                nc.scalar.activation(act[:, t : t + step, :], dealt[:, at : at + step, :], SILU, bias=bias[:])
+            nc.scalar.activation(act[:], dealt[:, 2 * half : 2 * half + 2, :], SILU, bias=bias[:])
             acts[g, half] = act
 
         def turn(g, half, bank):

@@ -28,9 +28,9 @@ WINDOW2_AT = 4 * T - EDGE
 WINDOW1_AT = WINDOW2_AT + T
 PLANES2_AT = WINDOW2_AT + 2 * EDGE
 EARLY = 2 * SLICE
-W_CODES_AT = PLANES2_AT + 4 * S
-W_SCALES_AT = W_CODES_AT + 2 * N
-BIAS_AT = W_SCALES_AT + N
+W_CODES_AT = WINDOW2_AT + EDGE
+BIAS_AT = W_CODES_AT + 2 * N
+W_SCALES_AT = PLANES2_AT + 4 * S
 TAB_WORDS_AT = WINDOW1_AT + T - EDGE
 
 
@@ -60,11 +60,6 @@ def tile_list_tab48_tm_silu_kernel(tc, tab, w4_words, w4_scales, tab2, u, b, off
         window2 = shared.tile([P, T // 4], I32, name="window2", offset=WINDOW2_AT, align_bytes=64)
         window1 = shared.tile([P, T // 4], I32, name="window1", offset=WINDOW1_AT, align_bytes=64)
 
-        seed = keep.tile([P, 1], F32, name="seed", tag="pair0_words")
-        warm = keep.tile([P, 1], F32, name="warm", tag="u_rows")
-        nc.gpsimd.memset(seed[:], 0.0)
-        nc.scalar.activation(warm[:], seed[:], SILU)
-
         nc.vector.memset(window1[:], 0)
         nc.vector.memset(window2[0:32, :], 0)
         nc.vector.memset(window2[96:128, :], 0)
@@ -91,6 +86,10 @@ def tile_list_tab48_tm_silu_kernel(tc, tab, w4_words, w4_scales, tab2, u, b, off
 
         scales2 = keep.tile([P, S], U8, name="scales2", align_bytes=64)
         gather(scales2[:], window2[:].bitcast(U8), list2, 0, S)
+        w_codes = shared.tile([P, 2 * N], U8, name="w_codes", offset=W_CODES_AT, align_bytes=64)
+        nc.sync.dma_start(out=w_codes[:].bitcast(I32), in_=w4_words[0].bitcast(I32))
+        bias = shared.tile([P, 1], F32, name="bias", offset=BIAS_AT, align_bytes=64)
+        nc.sync.dma_start(out=bias[:], in_=b.rearrange("(p o) -> p o", o=1))
         pair1_words = shared.tile([P, T], I32, name="pair1_words", offset=0, align_bytes=64)
         load_words(pair1_words, tab2[1:2])
         plane1 = keep.tile([P, S], U8, name="plane1", align_bytes=64)
@@ -113,12 +112,6 @@ def tile_list_tab48_tm_silu_kernel(tc, tab, w4_words, w4_scales, tab2, u, b, off
             return late[:, SLICE * at + first - EARLY : SLICE * at + first - EARLY + count]
 
         move_scale_rows(early, 0, EARLY)
-        w_codes = shared.tile([P, 2 * N], U8, name="w_codes", offset=W_CODES_AT, align_bytes=64)
-        nc.sync.dma_start(out=w_codes[:].bitcast(I32), in_=w4_words[0].bitcast(I32))
-        bias = shared.tile([P, 1], F32, name="bias", offset=BIAS_AT, align_bytes=64)
-        nc.sync.dma_start(out=bias[:], in_=b.rearrange("(p o) -> p o", o=1))
-        tab_words = shared.tile([P, T], I32, name="tab_words", offset=TAB_WORDS_AT, align_bytes=64)
-        load_words(tab_words, tab[0:1])
         w_scales = shared.tile([P, N], U8, name="w_scales", offset=W_SCALES_AT, align_bytes=64)
 
         def load_w_scales(quads):
@@ -128,7 +121,10 @@ def tile_list_tab48_tm_silu_kernel(tc, tab, w4_words, w4_scales, tab2, u, b, off
                     in_=w4_scales[0, 4 * quad : 4 * quad + 4, :].bitcast(I32),
                 )
 
-        load_w_scales(QUADRANTS[:3])
+        load_w_scales(QUADRANTS[:1])
+        tab_words = shared.tile([P, T], I32, name="tab_words", offset=TAB_WORDS_AT, align_bytes=64)
+        load_words(tab_words, tab[0:1])
+        load_w_scales(QUADRANTS[1:3])
         move_scale_rows(late, EARLY, SLICE)
         load_w_scales(QUADRANTS[3:])
 

@@ -128,36 +128,18 @@ def tile_list_tab48_tm_silu_kernel(tc, tab, w4_words, w4_scales, tab2, u, b, off
         move_scale_rows(late, EARLY, SLICE)
         load_w_scales(QUADRANTS[3:])
 
-        spread = psum.tile([P, N], F32, name="spread", tag="spare1")
-        nc.tensor.transpose(spread[:], bias[:].to_broadcast([P, P]), ident[:])
-        bias_rows = keep.tile([P, N], F32, name="bias_rows")
-        nc.scalar.copy(bias_rows[:], spread[:])
-
         u_grouped = keep.tile([P, 4, N, 4], BF16, name="u_grouped", align_bytes=64)
         nc.scalar.copy(out=u_grouped[:], in_=u_rows[:].rearrange("p a i n -> p a n i"))
         u_codes = keep.tile([P, 4 * N], U32, name="u_codes", align_bytes=64)
         u_scales = keep.tile([P, 4 * N], U8, name="u_scales", align_bytes=64)
 
-        acc = [psum.tile([P, SLICE], F32, name=f"acc{g}", tag=f"acc{g}") for g in range(2)]
-        last = [psum.tile([P, N], F32, name=f"last{t}", tag=f"last{t}") for t in range(4)]
+        acc = [psum.tile([P, SLICE], F32, name=f"acc{g}", tag=f"acc{g}") for g in range(SLICES)]
 
-        def multiply(s, codes, width, scales, w, w_scale, fmt, w_fmt, start, stop):
-            if s < 2:
-                nc.tensor.matmul_mx(
-                    out=acc[s][:], lhsT=w.bitcast(w_fmt), lhsT_scale=w_scale, rhs=codes.bitcast(fmt), rhs_scale=scales,
-                    start=start, stop=stop,
-                )
-                return
-            for t in range(4):
-                nc.tensor.matmul_mx(
-                    out=last[t][:],
-                    lhsT=codes[:, width * P * t : width * P * (t + 1)].bitcast(fmt),
-                    lhsT_scale=scales[:, P * t : P * (t + 1)],
-                    rhs=w.bitcast(w_fmt),
-                    rhs_scale=w_scale,
-                    start=start,
-                    stop=stop,
-                )
+        def multiply(s, codes, scales, w, w_scale, fmt, w_fmt, start, stop):
+            nc.tensor.matmul_mx(
+                out=acc[s][:], lhsT=w.bitcast(w_fmt), lhsT_scale=w_scale, rhs=codes.bitcast(fmt), rhs_scale=scales,
+                start=start, stop=stop,
+            )
 
         def tab2_pass(a, s):
             if a < 2:
@@ -165,14 +147,14 @@ def tile_list_tab48_tm_silu_kernel(tc, tab, w4_words, w4_scales, tab2, u, b, off
             else:
                 codes = parted1[s][:, 2 * SLICE * (a - 2) : 2 * SLICE * (a - 1)]
             cols = slice(N * a, N * (a + 1))
-            multiply(s, codes, 2, plane_of(a, SLICE * s, SLICE), u_codes[:, cols], u_scales[:, cols], FP4X4, FP8X4, a == 0, False)
+            multiply(s, codes, plane_of(a, SLICE * s, SLICE), u_codes[:, cols], u_scales[:, cols], FP4X4, FP8X4, a == 0, False)
 
         def tab_pass(s):
             cols = slice(SLICE * s, SLICE * (s + 1))
-            multiply(s, tab_codes[s][:], 1, plane1[:, cols], w_codes[:], w_scales[:], FP8X4, FP4X4, False, True)
+            multiply(s, tab_codes[s][:], plane1[:, cols], w_codes[:], w_scales[:], FP8X4, FP4X4, False, True)
 
         def tab_gather(s):
-            tab_codes[s] = keep.tile([P, SLICE], U32, name=f"tab_codes{s}", align_bytes=64)
+            tab_codes[s] = keep.tile([P, SLICE], U32, name=f"tab_codes{s}", tag=f"tab_codes{s % 2}", align_bytes=64)
             gather(tab_codes[s][:], tab_words[:].bitcast(U32), list1, SLICE * s, SLICE)
 
         pairs0 = keep.tile([P, S], U32, name="pairs0", align_bytes=64)
@@ -207,50 +189,49 @@ def tile_list_tab48_tm_silu_kernel(tc, tab, w4_words, w4_scales, tab2, u, b, off
             tab_gather(s)
         staged = keep.tile([P, S // P, N], F32, name="staged")
 
-        acts = {}
+        acts = [keep.tile([P, 4, P], F32, name=f"act{g}") for g in range(SLICES)]
 
-        def activate(g, half):
-            act = keep.tile([P, 2, P], F32, name=f"act{g}{half}")
-            dealt = acc[g][:].rearrange("n (p t) -> n t p", p=P)
-            nc.scalar.activation(act[:], dealt[:, 2 * half : 2 * half + 2, :], SILU, bias=bias[:])
-            acts[g, half] = act
+        def activate(g, first, count):
+            half, t = divmod(first, 2)
+            dealt = acc[g][:, 2 * P * half : 2 * P * (half + 1)].rearrange("n (p t) -> n t p", p=P)
+            nc.scalar.activation(acts[g][:, first : first + count, :], dealt[:, t : t + count, :], SILU, bias=bias[:])
 
-        def turn(g, half, bank):
-            turned = psum.tile([P, 2, N], F32, name=f"turned{g}{half}", tag=bank)
-            for t in range(2):
-                nc.tensor.transpose(turned[:, t, :], acts[g, half][:, t, :], ident[:])
+        def turn(g, first, count, bank):
+            turned = psum.tile([P, count, N], F32, name=f"turned{g}{first}", tag=bank)
+            for t in range(count):
+                nc.tensor.transpose(turned[:, t, :], acts[g][:, first + t, :], ident[:])
             return turned
 
-        def leave(g, half, turned, copy_out):
+        def store(g, half):
             at = 4 * g + 2 * half
-            copy_out(staged[:, at : at + 2, :], turned[:])
-            rows = out[SLICE * g : SLICE * (g + 1), :].rearrange("(p t) n -> p t n", p=P)
-            nc.sync.dma_start(out=rows[:, 2 * half : 2 * half + 2, :], in_=staged[:, at : at + 2, :])
+            rows = out[P * at : P * (at + 2), :].rearrange("(p t) n -> p t n", p=P)
+            nc.sync.dma_start(out=rows, in_=staged[:, at : at + 2, :])
 
         tab2_pass(0, 2)
+        tab2_pass(1, 2)
         tab_pass(0)
         tab_gather(2)
-        tab2_pass(1, 2)
         tab2_pass(2, 2)
-        tab_pass(1)
-        for g in range(2):
-            for half in range(2):
-                activate(g, half)
-        turned0 = [turn(0, 0, "spare0"), turn(0, 1, "spare1")]
         tab2_pass(3, 2)
-        turned1 = [turn(1, 0, "acc0")]
-        tab_pass(2)
-        turned1.append(turn(1, 1, "acc1"))
-        leave(0, 0, turned0[0], nc.vector.tensor_copy)
-        leave(0, 1, turned0[1], nc.scalar.copy)
+        tab_pass(1)
         for t in range(4):
-            shifted = keep.tile([P, N], F32, name=f"shifted{t}")
-            nc.vector.tensor_tensor(shifted[:], last[t][:], bias_rows[:], mybir.AluOpType.add)
-            if t == 0:
-                leave(1, 0, turned1[0], nc.scalar.copy)
-            nc.scalar.activation(staged[:, 8 + t, :], shifted[:], SILU)
-            if t % 2 == 1:
-                at = 7 + t
-                rows = out[P * at : P * (at + 2), :].rearrange("(t p) n -> p t n", p=P)
-                nc.sync.dma_start(out=rows, in_=staged[:, at : at + 2, :])
-        leave(1, 1, turned1[1], nc.vector.tensor_copy)
+            activate(0, t, 1)
+        activate(1, 0, 2)
+        activate(1, 2, 2)
+        turned = {(0, half): turn(0, 2 * half, 2, f"spare{half}") for half in range(2)}
+        tab_pass(2)
+        turned[1, 0] = turn(1, 0, 2, "spare2")
+        turned[1, 1] = turn(1, 2, 2, "spare3")
+        for t in range(4):
+            activate(2, t, 1)
+        turned[2, 0] = turn(2, 0, 2, "spare4")
+        ends = [turn(2, 2, 1, "acc0"), turn(2, 3, 1, "acc1")]
+        for g, half in ((0, 0), (0, 1), (1, 0), (1, 1)):
+            at = 4 * g + 2 * half
+            nc.vector.tensor_copy(staged[:, at : at + 2, :], turned[g, half][:])
+            store(g, half)
+        nc.scalar.copy(staged[:, 8:10, :], turned[2, 0][:])
+        store(2, 0)
+        nc.vector.tensor_copy(staged[:, 10:11, :], ends[0][:])
+        nc.scalar.copy(staged[:, 11:12, :], ends[1][:])
+        store(2, 1)

@@ -23,15 +23,14 @@ SLICES = S // SLICE
 LIST_COLS = S // 16
 QUADRANTS = (0, 2, 1, 3)
 
-EDGE = 512
-WINDOW2_AT = 4 * T - EDGE
-WINDOW1_AT = WINDOW2_AT + T
-PLANES2_AT = WINDOW2_AT + 2 * EDGE
+EDGE = 256
+WINDOW1_AT = 4 * T - EDGE
+WINDOW2_AT = WINDOW1_AT + T
+PLANE1_AT = WINDOW1_AT + EDGE
+PLANES2_AT = PLANE1_AT + S
 EARLY = 2 * SLICE
-W_CODES_AT = WINDOW2_AT + EDGE
-BIAS_AT = W_CODES_AT + 2 * N
-W_SCALES_AT = PLANES2_AT + 4 * S
-TAB_WORDS_AT = WINDOW1_AT + T - EDGE
+TAB_WORDS_AT = WINDOW2_AT + T - EDGE
+U_ROWS_AT = TAB_WORDS_AT + 4 * T
 
 
 def tile_list_tab48_tm_silu_kernel(tc, tab, w4_words, w4_scales, tab2, u, b, offs, offs2, out):
@@ -57,8 +56,8 @@ def tile_list_tab48_tm_silu_kernel(tc, tab, w4_words, w4_scales, tab2, u, b, off
 
         list2 = lists.tile([P, LIST_COLS], U16, name="list2")
         list1 = lists.tile([P, LIST_COLS], U16, name="list1")
-        window2 = shared.tile([P, T // 4], I32, name="window2", offset=WINDOW2_AT, align_bytes=64)
-        window1 = shared.tile([P, T // 4], I32, name="window1", offset=WINDOW1_AT, align_bytes=64)
+        window2 = shared.tile([P, T // 4], I32, name="window2", offset=WINDOW2_AT, align_bytes=256)
+        window1 = shared.tile([P, T // 4], I32, name="window1", offset=WINDOW1_AT, align_bytes=256)
 
         nc.vector.memset(window1[:], 0)
         nc.vector.memset(window2[0:32, :], 0)
@@ -67,33 +66,42 @@ def tile_list_tab48_tm_silu_kernel(tc, tab, w4_words, w4_scales, tab2, u, b, off
         nc.vector.memset(ident[:], 0.0)
         make_identity(nc, ident[:], nomemset=True)
 
+        nc.sync.dma_start(list1[:], offs)
+        nc.sync.dma_start(
+            out=window1[32:96:4, :], in_=tab[0:1, WORD_BYTES:].bitcast(I32).rearrange("o (q c) -> (o q) c", c=T // 4)
+        )
         nc.sync.dma_start(list2[:], offs2)
         for m in range(2):
             nc.sync.dma_start(
                 out=window2[32 + m : 96 : 2, :],
                 in_=tab2[m : m + 1, WORD_BYTES:].bitcast(I32).rearrange("o (h q c) -> (o q) h c", h=2, q=16),
             )
-        nc.sync.dma_start(list1[:], offs)
-        tab_scale_rows = tab[0:1, WORD_BYTES:].bitcast(I32).rearrange("o (q c) -> (o q) c", c=T // 4)
-        for quad in QUADRANTS:
-            nc.sync.dma_start(out=window1[32 * quad : 32 * quad + 4, :], in_=tab_scale_rows[4 * quad : 4 * quad + 4, :])
-        pair0_words = keep.tile([P, T], I32, name="pair0_words", tag="pair0_words")
+        pair0_words = keep.tile([P, T], I32, name="pair0_words", align_bytes=256)
         load_words(pair0_words, tab2[0:1])
-        u_rows = keep.tile([P, 4, 4, N], F32, name="u_rows", tag="u_rows")
+        u_rows = shared.tile([P, 4, 4, N], F32, name="u_rows", offset=U_ROWS_AT, align_bytes=256)
         nc.sync.dma_start(
             out=u_rows[:].rearrange("p a i n -> p a (i n)"), in_=u.rearrange("(a p i) n -> p a (i n)", a=4, i=4)
         )
+        w_codes = keep.tile([P, 2 * N], U8, name="w_codes", align_bytes=256)
+        nc.sync.dma_start(out=w_codes[:].bitcast(I32), in_=w4_words[0].bitcast(I32))
+        bias = keep.tile([P, 1], F32, name="bias")
+        nc.sync.dma_start(out=bias[:], in_=b.rearrange("(p o) -> p o", o=1))
 
+        scales1 = keep.tile([P, S], U8, name="scales1", align_bytes=64)
+        gather(scales1[:], window1[:].bitcast(U8), list1, 0, S)
+        plane1 = shared.tile([P, S], U8, name="plane1", offset=PLANE1_AT, align_bytes=64)
+        for quad in QUADRANTS:
+            nc.sync.dma_start(
+                out=plane1[32 * quad : 32 * quad + 4, :].bitcast(I32),
+                in_=scales1[32 + 16 * quad : 48 + 16 * quad : 4, :].bitcast(I32),
+            )
+        pair1_words = shared.tile([P, T], I32, name="pair1_words", offset=0, align_bytes=256)
+        load_words(pair1_words, tab2[1:2])
         scales2 = keep.tile([P, S], U8, name="scales2", align_bytes=64)
         gather(scales2[:], window2[:].bitcast(U8), list2, 0, S)
-        w_codes = shared.tile([P, 2 * N], U8, name="w_codes", offset=W_CODES_AT, align_bytes=64)
-        nc.sync.dma_start(out=w_codes[:].bitcast(I32), in_=w4_words[0].bitcast(I32))
-        bias = shared.tile([P, 1], F32, name="bias", offset=BIAS_AT, align_bytes=64)
-        nc.sync.dma_start(out=bias[:], in_=b.rearrange("(p o) -> p o", o=1))
-        pair1_words = shared.tile([P, T], I32, name="pair1_words", offset=0, align_bytes=64)
-        load_words(pair1_words, tab2[1:2])
-        plane1 = keep.tile([P, S], U8, name="plane1", align_bytes=64)
-        gather(plane1[:], window1[:].bitcast(U8), list1, 0, S)
+
+        u_grouped = keep.tile([P, 4, N, 4], BF16, name="u_grouped", align_bytes=64)
+        nc.scalar.copy(out=u_grouped[:], in_=u_rows[:].rearrange("p a i n -> p a n i"))
 
         early = shared.tile([P, 4 * EARLY], U8, name="early", offset=PLANES2_AT, align_bytes=64)
         late = shared.tile([P, 4 * SLICE], U8, name="late", offset=PLANES2_AT + 4 * EARLY, align_bytes=64)
@@ -112,7 +120,7 @@ def tile_list_tab48_tm_silu_kernel(tc, tab, w4_words, w4_scales, tab2, u, b, off
             return late[:, SLICE * at + first - EARLY : SLICE * at + first - EARLY + count]
 
         move_scale_rows(early, 0, EARLY)
-        w_scales = shared.tile([P, N], U8, name="w_scales", offset=W_SCALES_AT, align_bytes=64)
+        w_scales = shared.tile([P, N], U8, name="w_scales", offset=U_ROWS_AT, align_bytes=64)
 
         def load_w_scales(quads):
             for quad in quads:
@@ -122,14 +130,12 @@ def tile_list_tab48_tm_silu_kernel(tc, tab, w4_words, w4_scales, tab2, u, b, off
                 )
 
         load_w_scales(QUADRANTS[:1])
-        tab_words = shared.tile([P, T], I32, name="tab_words", offset=TAB_WORDS_AT, align_bytes=64)
+        tab_words = shared.tile([P, T], I32, name="tab_words", offset=TAB_WORDS_AT, align_bytes=256)
         load_words(tab_words, tab[0:1])
         load_w_scales(QUADRANTS[1:3])
         move_scale_rows(late, EARLY, SLICE)
         load_w_scales(QUADRANTS[3:])
 
-        u_grouped = keep.tile([P, 4, N, 4], BF16, name="u_grouped", align_bytes=64)
-        nc.scalar.copy(out=u_grouped[:], in_=u_rows[:].rearrange("p a i n -> p a n i"))
         u_codes = keep.tile([P, 4 * N], U32, name="u_codes", align_bytes=64)
         u_scales = keep.tile([P, 4 * N], U8, name="u_scales", align_bytes=64)
 

@@ -23,14 +23,14 @@ SLICES = S // SLICE
 LIST_COLS = S // 16
 QUADRANTS = (0, 2, 1, 3)
 
-EDGE = 256
-WINDOW1_AT = 4 * T - EDGE
-WINDOW2_AT = WINDOW1_AT + T
-PLANE1_AT = WINDOW1_AT + EDGE
-PLANES2_AT = PLANE1_AT + S
+EDGE = 128
+WINDOW2_AT = 4 * T - EDGE
+WINDOW1_AT = WINDOW2_AT + T
+W_SCALES_AT = WINDOW2_AT + EDGE
+PLANES2_AT = W_SCALES_AT + N
 EARLY = 2 * SLICE
-TAB_WORDS_AT = WINDOW2_AT + T - EDGE
-U_ROWS_AT = TAB_WORDS_AT + 4 * T
+PLANE1_AT = PLANES2_AT + 4 * S
+TAB_WORDS_AT = WINDOW1_AT + T - EDGE
 
 
 def tile_list_tab48_tm_silu_kernel(tc, tab, w4_words, w4_scales, tab2, u, b, offs, offs2, out):
@@ -56,8 +56,8 @@ def tile_list_tab48_tm_silu_kernel(tc, tab, w4_words, w4_scales, tab2, u, b, off
 
         list2 = lists.tile([P, LIST_COLS], U16, name="list2")
         list1 = lists.tile([P, LIST_COLS], U16, name="list1")
-        window2 = shared.tile([P, T // 4], I32, name="window2", offset=WINDOW2_AT, align_bytes=256)
-        window1 = shared.tile([P, T // 4], I32, name="window1", offset=WINDOW1_AT, align_bytes=256)
+        window2 = shared.tile([P, T // 4], I32, name="window2", offset=WINDOW2_AT, align_bytes=64)
+        window1 = shared.tile([P, T // 4], I32, name="window1", offset=WINDOW1_AT, align_bytes=64)
 
         nc.vector.memset(window1[:], 0)
         nc.vector.memset(window2[0:32, :], 0)
@@ -66,19 +66,19 @@ def tile_list_tab48_tm_silu_kernel(tc, tab, w4_words, w4_scales, tab2, u, b, off
         nc.vector.memset(ident[:], 0.0)
         make_identity(nc, ident[:], nomemset=True)
 
-        nc.sync.dma_start(list1[:], offs)
-        nc.sync.dma_start(
-            out=window1[32:96:4, :], in_=tab[0:1, WORD_BYTES:].bitcast(I32).rearrange("o (q c) -> (o q) c", c=T // 4)
-        )
         nc.sync.dma_start(list2[:], offs2)
         for m in range(2):
             nc.sync.dma_start(
                 out=window2[32 + m : 96 : 2, :],
                 in_=tab2[m : m + 1, WORD_BYTES:].bitcast(I32).rearrange("o (h q c) -> (o q) h c", h=2, q=16),
             )
+        nc.sync.dma_start(list1[:], offs)
+        nc.sync.dma_start(
+            out=window1[32:96:4, :], in_=tab[0:1, WORD_BYTES:].bitcast(I32).rearrange("o (q c) -> (o q) c", c=T // 4)
+        )
         pair0_words = keep.tile([P, T], I32, name="pair0_words", align_bytes=256)
         load_words(pair0_words, tab2[0:1])
-        u_rows = shared.tile([P, 4, 4, N], F32, name="u_rows", offset=U_ROWS_AT, align_bytes=256)
+        u_rows = keep.tile([P, 4, 4, N], F32, name="u_rows", align_bytes=256)
         nc.sync.dma_start(
             out=u_rows[:].rearrange("p a i n -> p a (i n)"), in_=u.rearrange("(a p i) n -> p a (i n)", a=4, i=4)
         )
@@ -87,18 +87,18 @@ def tile_list_tab48_tm_silu_kernel(tc, tab, w4_words, w4_scales, tab2, u, b, off
         bias = keep.tile([P, 1], F32, name="bias")
         nc.sync.dma_start(out=bias[:], in_=b.rearrange("(p o) -> p o", o=1))
 
-        scales1 = keep.tile([P, S], U8, name="scales1", align_bytes=64)
-        gather(scales1[:], window1[:].bitcast(U8), list1, 0, S)
-        plane1 = shared.tile([P, S], U8, name="plane1", offset=PLANE1_AT, align_bytes=64)
+        scales2 = keep.tile([P, S], U8, name="scales2", align_bytes=64)
+        gather(scales2[:], window2[:].bitcast(U8), list2, 0, S)
+        w_scales = shared.tile([P, N], U8, name="w_scales", offset=W_SCALES_AT, align_bytes=64)
         for quad in QUADRANTS:
             nc.sync.dma_start(
-                out=plane1[32 * quad : 32 * quad + 4, :].bitcast(I32),
-                in_=scales1[32 + 16 * quad : 48 + 16 * quad : 4, :].bitcast(I32),
+                out=w_scales[32 * quad : 32 * quad + 4, :].bitcast(I32),
+                in_=w4_scales[0, 4 * quad : 4 * quad + 4, :].bitcast(I32),
             )
         pair1_words = shared.tile([P, T], I32, name="pair1_words", offset=0, align_bytes=256)
         load_words(pair1_words, tab2[1:2])
-        scales2 = keep.tile([P, S], U8, name="scales2", align_bytes=64)
-        gather(scales2[:], window2[:].bitcast(U8), list2, 0, S)
+        scales1 = keep.tile([P, S], U8, name="scales1", align_bytes=64)
+        gather(scales1[:], window1[:].bitcast(U8), list1, 0, S)
 
         u_grouped = keep.tile([P, 4, N, 4], BF16, name="u_grouped", align_bytes=64)
         nc.scalar.copy(out=u_grouped[:], in_=u_rows[:].rearrange("p a i n -> p a n i"))
@@ -120,21 +120,20 @@ def tile_list_tab48_tm_silu_kernel(tc, tab, w4_words, w4_scales, tab2, u, b, off
             return late[:, SLICE * at + first - EARLY : SLICE * at + first - EARLY + count]
 
         move_scale_rows(early, 0, EARLY)
-        w_scales = shared.tile([P, N], U8, name="w_scales", offset=U_ROWS_AT, align_bytes=64)
+        plane1 = shared.tile([P, S], U8, name="plane1", offset=PLANE1_AT, align_bytes=64)
 
-        def load_w_scales(quads):
+        def move_tab_rows(quads):
             for quad in quads:
                 nc.sync.dma_start(
-                    out=w_scales[32 * quad : 32 * quad + 4, :].bitcast(I32),
-                    in_=w4_scales[0, 4 * quad : 4 * quad + 4, :].bitcast(I32),
+                    out=plane1[32 * quad : 32 * quad + 4, :].bitcast(I32),
+                    in_=scales1[32 + 16 * quad : 48 + 16 * quad : 4, :].bitcast(I32),
                 )
 
-        load_w_scales(QUADRANTS[:1])
+        move_tab_rows(QUADRANTS[:1])
         tab_words = shared.tile([P, T], I32, name="tab_words", offset=TAB_WORDS_AT, align_bytes=256)
         load_words(tab_words, tab[0:1])
-        load_w_scales(QUADRANTS[1:3])
         move_scale_rows(late, EARLY, SLICE)
-        load_w_scales(QUADRANTS[3:])
+        move_tab_rows(QUADRANTS[1:])
 
         u_codes = keep.tile([P, 4 * N], U32, name="u_codes", align_bytes=64)
         u_scales = keep.tile([P, 4 * N], U8, name="u_scales", align_bytes=64)

@@ -18,8 +18,8 @@ SILU = mybir.ActivationFunctionType.Silu
 
 P = 128
 WORD_BYTES = 512 * T
-SLICE = 512
-SLICES = S // SLICE
+UNIT = 256
+UNITS = S // UNIT
 LIST_COLS = S // 16
 QUADRANTS = (0, 2, 1, 3)
 
@@ -28,7 +28,6 @@ WINDOW2_AT = 4 * T - EDGE
 WINDOW1_AT = WINDOW2_AT + T
 W_SCALES_AT = WINDOW2_AT + EDGE
 PLANES2_AT = W_SCALES_AT + N
-EARLY = 2 * SLICE
 PLANE1_AT = PLANES2_AT + 4 * S
 TAB_WORDS_AT = WINDOW1_AT + T - EDGE
 
@@ -76,167 +75,148 @@ def tile_list_tab48_tm_silu_kernel(tc, tab, w4_words, w4_scales, tab2, u, b, off
         nc.sync.dma_start(
             out=window1[32:96:4, :], in_=tab[0:1, WORD_BYTES:].bitcast(I32).rearrange("o (q c) -> (o q) c", c=T // 4)
         )
+        w_codes = keep.tile([P, 2 * N], U8, name="w_codes", align_bytes=256)
+        nc.sync.dma_start(out=w_codes[:].bitcast(I32), in_=w4_words[0].bitcast(I32))
+        bias = keep.tile([P, 1], F32, name="bias")
+        nc.sync.dma_start(out=bias[:], in_=b.rearrange("(p o) -> p o", o=1))
         pair0_words = keep.tile([P, T], I32, name="pair0_words", align_bytes=256)
         load_words(pair0_words, tab2[0:1])
         u_rows = keep.tile([P, 4, 4, N], F32, name="u_rows", align_bytes=256)
         nc.sync.dma_start(
             out=u_rows[:].rearrange("p a i n -> p a (i n)"), in_=u.rearrange("(a p i) n -> p a (i n)", a=4, i=4)
         )
-        w_codes = keep.tile([P, 2 * N], U8, name="w_codes", align_bytes=256)
-        nc.sync.dma_start(out=w_codes[:].bitcast(I32), in_=w4_words[0].bitcast(I32))
-        bias = keep.tile([P, 1], F32, name="bias")
-        nc.sync.dma_start(out=bias[:], in_=b.rearrange("(p o) -> p o", o=1))
 
         scales2 = keep.tile([P, S], U8, name="scales2", align_bytes=64)
         gather(scales2[:], window2[:].bitcast(U8), list2, 0, S)
         w_scales = shared.tile([P, N], U8, name="w_scales", offset=W_SCALES_AT, align_bytes=64)
-        for quad in QUADRANTS:
+        planes2 = [
+            shared.tile([P, 2 * S], U8, name=f"planes2_{m}", offset=PLANES2_AT + 2 * S * m, align_bytes=64)
+            for m in range(2)
+        ]
+        plane1 = shared.tile([P, S], U8, name="plane1", offset=PLANE1_AT, align_bytes=64)
+
+        def load_w_scales(quads):
+            for quad in quads:
+                nc.sync.dma_start(
+                    out=w_scales[32 * quad : 32 * quad + 4, :].bitcast(I32),
+                    in_=w4_scales[0, 4 * quad : 4 * quad + 4, :].bitcast(I32),
+                )
+
+        def move_tab2_rows(m):
+            for quad in QUADRANTS:
+                nc.sync.dma_start(
+                    out=planes2[m][32 * quad : 32 * quad + 4, :].bitcast(I32).rearrange("r (h c) -> r h c", h=2),
+                    in_=scales2[32 + 16 * quad + m : 48 + 16 * quad : 2, :].bitcast(I32),
+                )
+
+        def move_tab_rows(quad, first, last):
             nc.sync.dma_start(
-                out=w_scales[32 * quad : 32 * quad + 4, :].bitcast(I32),
-                in_=w4_scales[0, 4 * quad : 4 * quad + 4, :].bitcast(I32),
+                out=plane1[32 * quad : 32 * quad + 4, first:last].bitcast(I32),
+                in_=scales1[32 + 16 * quad : 48 + 16 * quad : 4, first:last].bitcast(I32),
             )
+
+        move_tab2_rows(0)
+        load_w_scales(QUADRANTS[:2])
         pair1_words = shared.tile([P, T], I32, name="pair1_words", offset=0, align_bytes=256)
         load_words(pair1_words, tab2[1:2])
         scales1 = keep.tile([P, S], U8, name="scales1", align_bytes=64)
         gather(scales1[:], window1[:].bitcast(U8), list1, 0, S)
+        move_tab2_rows(1)
+        load_w_scales(QUADRANTS[2:])
+        tab_words = shared.tile([P, T], I32, name="tab_words", offset=TAB_WORDS_AT, align_bytes=256)
+        load_words(tab_words, tab[0:1])
+        for quad in QUADRANTS[:3]:
+            move_tab_rows(quad, 0, S)
+        for unit in range(UNITS):
+            move_tab_rows(QUADRANTS[3], UNIT * unit, UNIT * (unit + 1))
 
         u_grouped = keep.tile([P, 4, N, 4], BF16, name="u_grouped", align_bytes=64)
         nc.scalar.copy(out=u_grouped[:], in_=u_rows[:].rearrange("p a i n -> p a n i"))
 
-        early = shared.tile([P, 4 * EARLY], U8, name="early", offset=PLANES2_AT, align_bytes=64)
-        late = shared.tile([P, 4 * SLICE], U8, name="late", offset=PLANES2_AT + 4 * EARLY, align_bytes=64)
-
-        def move_scale_rows(planes, first, count):
-            for quad in QUADRANTS:
-                nc.sync.dma_start(
-                    out=planes[32 * quad : 32 * quad + 4, :].bitcast(I32).rearrange("r (a c) -> r a c", a=4),
-                    in_=scales2[32 + 16 * quad : 48 + 16 * quad, first : first + count].bitcast(I32),
-                )
-
-        def plane_of(a, first, count):
-            at = 2 * (a % 2) + a // 2
-            if first < EARLY:
-                return early[:, EARLY * at + first : EARLY * at + first + count]
-            return late[:, SLICE * at + first - EARLY : SLICE * at + first - EARLY + count]
-
-        move_scale_rows(early, 0, EARLY)
-        plane1 = shared.tile([P, S], U8, name="plane1", offset=PLANE1_AT, align_bytes=64)
-
-        def move_tab_rows(quads):
-            for quad in quads:
-                nc.sync.dma_start(
-                    out=plane1[32 * quad : 32 * quad + 4, :].bitcast(I32),
-                    in_=scales1[32 + 16 * quad : 48 + 16 * quad : 4, :].bitcast(I32),
-                )
-
-        move_tab_rows(QUADRANTS[:1])
-        tab_words = shared.tile([P, T], I32, name="tab_words", offset=TAB_WORDS_AT, align_bytes=256)
-        load_words(tab_words, tab[0:1])
-        move_scale_rows(late, EARLY, SLICE)
-        move_tab_rows(QUADRANTS[1:])
-
         u_codes = keep.tile([P, 4 * N], U32, name="u_codes", align_bytes=64)
         u_scales = keep.tile([P, 4 * N], U8, name="u_scales", align_bytes=64)
 
-        acc = [psum.tile([P, SLICE], F32, name=f"acc{g}", tag=f"acc{g}") for g in range(SLICES)]
+        acc = [psum.tile([P, UNIT], F32, name=f"acc{g}", tag=f"acc{g}") for g in range(UNITS)]
+        pairs = [keep.tile([P, S], U32, name=f"pairs{m}", align_bytes=64) for m in range(2)]
+        parted = [keep.tile([P, 4 * S], U8, name=f"parted{m}", align_bytes=64) for m in range(2)]
 
-        def multiply(s, codes, scales, w, w_scale, fmt, w_fmt, start, stop):
+        def multiply(g, codes, scales, w, w_scale, fmt, w_fmt, start, stop):
             nc.tensor.matmul_mx(
-                out=acc[s][:], lhsT=w.bitcast(w_fmt), lhsT_scale=w_scale, rhs=codes.bitcast(fmt), rhs_scale=scales,
+                out=acc[g][:], lhsT=w.bitcast(w_fmt), lhsT_scale=w_scale, rhs=codes.bitcast(fmt), rhs_scale=scales,
                 start=start, stop=stop,
             )
 
-        def tab2_pass(a, s):
-            if a < 2:
-                codes = parted0[:, 2 * (S * a + SLICE * s) : 2 * (S * a + SLICE * (s + 1))]
-            else:
-                codes = parted1[s][:, 2 * SLICE * (a - 2) : 2 * SLICE * (a - 1)]
-            cols = slice(N * a, N * (a + 1))
-            multiply(s, codes, plane_of(a, SLICE * s, SLICE), u_codes[:, cols], u_scales[:, cols], FP4X4, FP8X4, a == 0, False)
+        def tab2_passes(m, first, count):
+            for h in range(2):
+                cols = slice(N * (2 * m + h), N * (2 * m + h + 1))
+                for item in range(first, first + count, UNIT):
+                    codes = parted[m][:, 2 * (S * h + item) : 2 * (S * h + item + UNIT)]
+                    multiply(
+                        item // UNIT, codes, planes2[m][:, S * h + item : S * h + item + UNIT], u_codes[:, cols], u_scales[:, cols],
+                        FP4X4, FP8X4, m == 0 and h == 0, False,
+                    )
 
-        def tab_pass(s):
-            cols = slice(SLICE * s, SLICE * (s + 1))
-            multiply(s, tab_codes[s][:], plane1[:, cols], w_codes[:], w_scales[:], FP8X4, FP4X4, False, True)
-
-        def tab_gather(s):
-            tab_codes[s] = keep.tile([P, SLICE], U32, name=f"tab_codes{s}", tag=f"tab_codes{s % 2}", align_bytes=64)
-            gather(tab_codes[s][:], tab_words[:].bitcast(U32), list1, SLICE * s, SLICE)
-
-        pairs0 = keep.tile([P, S], U32, name="pairs0", align_bytes=64)
         for first in (0, S // 2):
-            gather(pairs0[:, first : first + S // 2], pair0_words[:].bitcast(U32), list2, first, S // 2)
-        parted0 = keep.tile([P, 4 * S], U8, name="parted0", align_bytes=64)
-        tab_codes = {}
+            gather(pairs[0][:, first : first + S // 2], pair0_words[:].bitcast(U32), list2, first, S // 2)
         for first in (0, S // 2):
-            part(parted0, pairs0, first, S // 2)
+            part(parted[0], pairs[0], first, S // 2)
         nc.vector.quantize_mx(
             out=u_codes[:].bitcast(FP8X4), scales=u_scales[:], in_=u_grouped[:].rearrange("p a n i -> p (a n i)")
         )
-        for s in range(2):
-            for a in range(2):
-                tab2_pass(a, s)
+        tab2_passes(0, 0, S)
 
-        parted1 = [keep.tile([P, 4 * SLICE], U8, name=f"parted1_{s}", align_bytes=64) for s in range(SLICES)]
-        pairs1 = [keep.tile([P, SLICE], U32, name=f"pairs1_{s}", align_bytes=64) for s in range(SLICES)]
-        order = (0, 2, 1)
-        for step in range(SLICES + 1):
-            if step < SLICES:
-                s = order[step]
-                gather(pairs1[s][:], pair1_words[:].bitcast(U32), list2, SLICE * s, SLICE)
+        third = S // 3
+        for step in range(4):
+            if step < 3:
+                first = third * step
+                gather(pairs[1][:, first : first + third], pair1_words[:].bitcast(U32), list2, first, third)
             if step > 0:
-                s = order[step - 1]
-                part(parted1[s], pairs1[s], 0, SLICE)
-                if s < 2:
-                    for a in (2, 3):
-                        tab2_pass(a, s)
+                first = third * (step - 1)
+                part(parted[1], pairs[1], first, third)
+                tab2_passes(1, first, third)
 
-        for s in range(2):
-            tab_gather(s)
+        acts = keep.tile([P, S // P, P], F32, name="acts")
         staged = keep.tile([P, S // P, N], F32, name="staged")
 
-        acts = [keep.tile([P, 4, P], F32, name=f"act{g}") for g in range(SLICES)]
+        def close(unit):
+            codes = keep.tile([P, UNIT], U32, name=f"tab_codes{unit}", align_bytes=64)
+            gather(codes[:], tab_words[:].bitcast(U32), list1, UNIT * unit, UNIT)
+            cols = slice(UNIT * unit, UNIT * (unit + 1))
+            multiply(unit, codes[:], plane1[:, cols], w_codes[:], w_scales[:], FP8X4, FP4X4, False, True)
 
-        def activate(g, first, count):
-            half, t = divmod(first, 2)
-            dealt = acc[g][:, 2 * P * half : 2 * P * (half + 1)].rearrange("n (p t) -> n t p", p=P)
-            nc.scalar.activation(acts[g][:, first : first + count, :], dealt[:, t : t + count, :], SILU, bias=bias[:])
+        def activate(unit, t, count):
+            dealt = acc[unit][:].rearrange("n (p t) -> n t p", p=P)
+            rows = slice(2 * unit + t, 2 * unit + t + count)
+            nc.scalar.activation(acts[:, rows, :], dealt[:, t : t + count, :], SILU, bias=bias[:])
 
-        def turn(g, first, count, bank):
-            turned = psum.tile([P, count, N], F32, name=f"turned{g}{first}", tag=bank)
+        def turn(first, count, bank):
+            turned = psum.tile([P, count, N], F32, name=f"turned{first}", tag=bank)
             for t in range(count):
-                nc.tensor.transpose(turned[:, t, :], acts[g][:, first + t, :], ident[:])
+                nc.tensor.transpose(turned[:, t, :], acts[:, first + t, :], ident[:])
             return turned
 
-        def store(g, half):
-            at = 4 * g + 2 * half
-            rows = out[P * at : P * (at + 2), :].rearrange("(p t) n -> p t n", p=P)
-            nc.sync.dma_start(out=rows, in_=staged[:, at : at + 2, :])
+        def store(unit):
+            rows = out[UNIT * unit : UNIT * (unit + 1), :].rearrange("(p t) n -> p t n", p=P)
+            nc.sync.dma_start(out=rows, in_=staged[:, 2 * unit : 2 * unit + 2, :])
 
-        tab2_pass(0, 2)
-        tab2_pass(1, 2)
-        tab_pass(0)
-        tab_gather(2)
-        tab2_pass(2, 2)
-        tab2_pass(3, 2)
-        tab_pass(1)
-        for t in range(4):
-            activate(0, t, 1)
-        activate(1, 0, 2)
-        activate(1, 2, 2)
-        turned = {(0, half): turn(0, 2 * half, 2, f"spare{half}") for half in range(2)}
-        tab_pass(2)
-        turned[1, 0] = turn(1, 0, 2, "spare2")
-        turned[1, 1] = turn(1, 2, 2, "spare3")
-        for t in range(4):
-            activate(2, t, 1)
-        turned[2, 0] = turn(2, 0, 2, "spare4")
-        ends = [turn(2, 2, 1, "acc0"), turn(2, 3, 1, "acc1")]
-        for g, half in ((0, 0), (0, 1), (1, 0), (1, 1)):
-            at = 4 * g + 2 * half
-            nc.vector.tensor_copy(staged[:, at : at + 2, :], turned[g, half][:])
-            store(g, half)
-        nc.scalar.copy(staged[:, 8:10, :], turned[2, 0][:])
-        store(2, 0)
-        nc.vector.tensor_copy(staged[:, 10:11, :], ends[0][:])
-        nc.scalar.copy(staged[:, 11:12, :], ends[1][:])
-        store(2, 1)
+        def leave(unit, copy):
+            copy(staged[:, 2 * unit : 2 * unit + 2, :], turned[unit][:])
+            store(unit)
+
+        turned = {}
+        banks = ("spare0", "spare1", "acc0", "acc1", "acc2")
+        on_scalar = (0, 1)
+        for unit in range(UNITS):
+            close(unit)
+        for unit in range(UNITS - 1):
+            activate(unit, 0, 2)
+            turned[unit] = turn(2 * unit, 2, banks[unit])
+            if unit - 1 in on_scalar:
+                leave(unit - 1, nc.scalar.copy)
+        activate(5, 0, 1)
+        activate(5, 1, 1)
+        for unit in (2, 3, 4):
+            leave(unit, nc.vector.tensor_copy)
+        nc.vector.tensor_copy(staged[:, 10:11, :], turn(10, 1, "acc3")[:])
+        nc.scalar.copy(staged[:, 11:12, :], turn(11, 1, "spare0")[:])
+        store(5)

@@ -15,11 +15,13 @@ U8 = mybir.dt.uint8
 FP8X4 = mybir.dt.float8_e4m3fn_x4
 FP4X4 = mybir.dt.float4_e2m1fn_x4
 SILU = mybir.ActivationFunctionType.Silu
+ADD = mybir.AluOpType.add
 
 P = 128
 WORD_BYTES = 512 * T
 UNIT = 256
 UNITS = S // UNIT
+TURNED = 4
 LIST_COLS = S // 16
 QUADRANTS = (0, 2, 1, 3)
 
@@ -136,24 +138,41 @@ def tile_list_tab48_tm_silu_kernel(tc, tab, w4_words, w4_scales, tab2, u, b, off
         u_codes = keep.tile([P, 4 * N], U32, name="u_codes", align_bytes=64)
         u_scales = keep.tile([P, 4 * N], U8, name="u_scales", align_bytes=64)
 
-        acc = [psum.tile([P, UNIT], F32, name=f"acc{g}", tag=f"acc{g}") for g in range(UNITS)]
+        spread = psum.tile([P, N], F32, name="spread", tag="spare")
+        nc.tensor.transpose(spread[:], bias[:].to_broadcast([P, P]), ident[:])
+        bias_rows = keep.tile([P, N], F32, name="bias_rows")
+        nc.scalar.copy(bias_rows[:], spread[:])
+
+        acc = [psum.tile([P, UNIT], F32, name=f"acc{g}", tag=f"acc{g}") for g in range(TURNED)]
+        both = psum.tile([P, 2, N], F32, name="both", tag="both")
+        last = [psum.tile([P, N], F32, name=f"end{t}", tag=f"end{t}") for t in range(2)]
+        ends = {(4, 0): both[:, 0, :], (4, 1): both[:, 1, :], (5, 0): last[0][:], (5, 1): last[1][:]}
         pairs = [keep.tile([P, S], U32, name=f"pairs{m}", align_bytes=64) for m in range(2)]
         parted = [keep.tile([P, 4 * S], U8, name=f"parted{m}", align_bytes=64) for m in range(2)]
 
-        def multiply(g, codes, scales, w, w_scale, fmt, w_fmt, start, stop):
-            nc.tensor.matmul_mx(
-                out=acc[g][:], lhsT=w.bitcast(w_fmt), lhsT_scale=w_scale, rhs=codes.bitcast(fmt), rhs_scale=scales,
-                start=start, stop=stop,
-            )
+        def multiply(unit, codes, width, scales, w, w_scale, fmt, w_fmt, start, stop):
+            if unit < TURNED:
+                nc.tensor.matmul_mx(
+                    out=acc[unit][:], lhsT=w.bitcast(w_fmt), lhsT_scale=w_scale, rhs=codes.bitcast(fmt),
+                    rhs_scale=scales, start=start, stop=stop,
+                )
+            else:
+                for t in range(2):
+                    nc.tensor.matmul_mx(
+                        out=ends[unit, t], lhsT=codes[:, width * P * t : width * P * (t + 1)].bitcast(fmt),
+                        lhsT_scale=scales[:, P * t : P * (t + 1)], rhs=w.bitcast(w_fmt), rhs_scale=w_scale,
+                        start=start and (unit == 5 or t == 0), stop=stop and (unit == 5 or t == 1),
+                    )
 
         def tab2_passes(m, first, count):
             for h in range(2):
                 cols = slice(N * (2 * m + h), N * (2 * m + h + 1))
                 for item in range(first, first + count, UNIT):
                     codes = parted[m][:, 2 * (S * h + item) : 2 * (S * h + item + UNIT)]
+                    scales = planes2[m][:, S * h + item : S * h + item + UNIT]
                     multiply(
-                        item // UNIT, codes, planes2[m][:, S * h + item : S * h + item + UNIT], u_codes[:, cols], u_scales[:, cols],
-                        FP4X4, FP8X4, m == 0 and h == 0, False,
+                        item // UNIT, codes, 2, scales, u_codes[:, cols], u_scales[:, cols], FP4X4, FP8X4,
+                        m == 0 and h == 0, False,
                     )
 
         for first in (0, S // 2):
@@ -182,7 +201,7 @@ def tile_list_tab48_tm_silu_kernel(tc, tab, w4_words, w4_scales, tab2, u, b, off
             codes = keep.tile([P, UNIT], U32, name=f"tab_codes{unit}", align_bytes=64)
             gather(codes[:], tab_words[:].bitcast(U32), list1, UNIT * unit, UNIT)
             cols = slice(UNIT * unit, UNIT * (unit + 1))
-            multiply(unit, codes[:], plane1[:, cols], w_codes[:], w_scales[:], FP8X4, FP4X4, False, True)
+            multiply(unit, codes[:], 1, plane1[:, cols], w_codes[:], w_scales[:], FP8X4, FP4X4, False, True)
 
         def activate(unit, t, count):
             dealt = acc[unit][:].rearrange("n (p t) -> n t p", p=P)
@@ -203,20 +222,25 @@ def tile_list_tab48_tm_silu_kernel(tc, tab, w4_words, w4_scales, tab2, u, b, off
             copy(staged[:, 2 * unit : 2 * unit + 2, :], turned[unit][:])
             store(unit)
 
+        def leave_upright(unit):
+            rows = out[UNIT * unit : UNIT * (unit + 1), :].rearrange("(t p) n -> p t n", p=P)
+            nc.sync.dma_start(out=rows, in_=staged[:, 2 * unit : 2 * unit + 2, :])
+
         turned = {}
-        banks = ("spare0", "spare1", "acc0", "acc1", "acc2")
-        on_scalar = (0, 1)
+        banks = ("spare", "acc0", "acc1", "acc2")
         for unit in range(UNITS):
             close(unit)
-        for unit in range(UNITS - 1):
+        for unit in range(TURNED):
             activate(unit, 0, 2)
             turned[unit] = turn(2 * unit, 2, banks[unit])
-            if unit - 1 in on_scalar:
+            if unit > 0:
                 leave(unit - 1, nc.scalar.copy)
-        activate(5, 0, 1)
-        activate(5, 1, 1)
-        for unit in (2, 3, 4):
-            leave(unit, nc.vector.tensor_copy)
-        nc.vector.tensor_copy(staged[:, 10:11, :], turn(10, 1, "acc3")[:])
-        nc.scalar.copy(staged[:, 11:12, :], turn(11, 1, "spare0")[:])
-        store(5)
+        nc.vector.tensor_tensor(acts[:, 8:10, :], both[:], bias_rows[:].unsqueeze(1).to_broadcast([P, 2, N]), ADD)
+        for t in range(2):
+            nc.vector.tensor_tensor(acts[:, 10 + t, :], ends[5, t], bias_rows[:], ADD)
+        nc.scalar.activation(staged[:, 8:10, :], acts[:, 8:10, :], SILU)
+        leave_upright(4)
+        for t in range(2):
+            nc.scalar.activation(staged[:, 10 + t, :], acts[:, 10 + t, :], SILU)
+        leave(3, nc.vector.tensor_copy)
+        leave_upright(5)

@@ -21,7 +21,7 @@ P = 128
 WORD_BYTES = 512 * T
 UNIT = 256
 UNITS = S // UNIT
-TURNED = 4
+TURNED = 3
 LIST_COLS = S // 16
 QUADRANTS = (0, 2, 1, 3)
 
@@ -144,9 +144,11 @@ def tile_list_tab48_tm_silu_kernel(tc, tab, w4_words, w4_scales, tab2, u, b, off
         nc.scalar.copy(bias_rows[:], spread[:])
 
         acc = [psum.tile([P, UNIT], F32, name=f"acc{g}", tag=f"acc{g}") for g in range(TURNED)]
-        both = psum.tile([P, 2, N], F32, name="both", tag="both")
+        both = {g: psum.tile([P, 2, N], F32, name=f"both{g}", tag=f"both{g}") for g in range(TURNED, UNITS - 1)}
         last = [psum.tile([P, N], F32, name=f"end{t}", tag=f"end{t}") for t in range(2)]
-        ends = {(4, 0): both[:, 0, :], (4, 1): both[:, 1, :], (5, 0): last[0][:], (5, 1): last[1][:]}
+        ends = {(g, t): both[g][:, t, :] for g in both for t in range(2)}
+        for t in range(2):
+            ends[UNITS - 1, t] = last[t][:]
         pairs = [keep.tile([P, S], U32, name=f"pairs{m}", align_bytes=64) for m in range(2)]
         parted = [keep.tile([P, 4 * S], U8, name=f"parted{m}", align_bytes=64) for m in range(2)]
 
@@ -227,7 +229,7 @@ def tile_list_tab48_tm_silu_kernel(tc, tab, w4_words, w4_scales, tab2, u, b, off
             nc.sync.dma_start(out=rows, in_=staged[:, 2 * unit : 2 * unit + 2, :])
 
         turned = {}
-        banks = ("spare", "acc0", "acc1", "acc2")
+        banks = ("spare", "acc0", "acc1")
         for unit in range(UNITS):
             close(unit)
         for unit in range(TURNED):
@@ -235,12 +237,13 @@ def tile_list_tab48_tm_silu_kernel(tc, tab, w4_words, w4_scales, tab2, u, b, off
             turned[unit] = turn(2 * unit, 2, banks[unit])
             if unit > 0:
                 leave(unit - 1, nc.scalar.copy)
-        nc.vector.tensor_tensor(acts[:, 8:10, :], both[:], bias_rows[:].unsqueeze(1).to_broadcast([P, 2, N]), ADD)
+        leave(TURNED - 1, nc.scalar.copy)
+        for unit in range(TURNED, UNITS - 1):
+            rows = slice(2 * unit, 2 * unit + 2)
+            nc.vector.tensor_tensor(acts[:, rows, :], both[unit][:], bias_rows[:].unsqueeze(1).to_broadcast([P, 2, N]), ADD)
+            nc.scalar.activation(staged[:, rows, :], acts[:, rows, :], SILU)
+            leave_upright(unit)
         for t in range(2):
             nc.vector.tensor_tensor(acts[:, 10 + t, :], ends[5, t], bias_rows[:], ADD)
-        nc.scalar.activation(staged[:, 8:10, :], acts[:, 8:10, :], SILU)
-        leave_upright(4)
-        for t in range(2):
             nc.scalar.activation(staged[:, 10 + t, :], acts[:, 10 + t, :], SILU)
-        leave(3, nc.vector.tensor_copy)
         leave_upright(5)

@@ -127,9 +127,14 @@ def tile_list_tab48_tm_silu_kernel(tc, tab, w4_words, w4_scales, tab2, u, b, off
         load_w_scales(QUADRANTS[2:])
         tab_words = shared.tile([P, T], I32, name="tab_words", offset=TAB_WORDS_AT, align_bytes=256)
         load_words(tab_words, tab[0:1])
-        for quad in QUADRANTS[:3]:
-            move_tab_rows(quad, 0, S)
-        for unit in range(UNITS):
+        move_tab_rows(QUADRANTS[0], 0, S)
+        for quad in QUADRANTS[1:3]:
+            move_tab_rows(quad, 0, 4 * UNIT)
+        for first, last in ((0, 1), (1, 3), (3, 4)):
+            move_tab_rows(QUADRANTS[3], UNIT * first, UNIT * last)
+        for quad in QUADRANTS[1:3]:
+            move_tab_rows(quad, 4 * UNIT, S)
+        for unit in (4, 5):
             move_tab_rows(QUADRANTS[3], UNIT * unit, UNIT * (unit + 1))
 
         u_grouped = keep.tile([P, 4, N, 4], BF16, name="u_grouped", align_bytes=64)
@@ -235,15 +240,17 @@ def tile_list_tab48_tm_silu_kernel(tc, tab, w4_words, w4_scales, tab2, u, b, off
         for unit in range(TURNED):
             activate(unit, 0, 2)
             turned[unit] = turn(2 * unit, 2, banks[unit])
-            if unit > 0:
-                leave(unit - 1, nc.scalar.copy)
-        leave(TURNED - 1, nc.scalar.copy)
+        for unit in range(TURNED):
+            leave(unit, nc.scalar.copy)
         for unit in range(TURNED, UNITS - 1):
-            rows = slice(2 * unit, 2 * unit + 2)
-            nc.vector.tensor_tensor(acts[:, rows, :], both[unit][:], bias_rows[:].unsqueeze(1).to_broadcast([P, 2, N]), ADD)
-            nc.scalar.activation(staged[:, rows, :], acts[:, rows, :], SILU)
+            for t, count in ((0, 1), (1, 1)) if unit == TURNED else ((0, 2),):
+                rows = slice(2 * unit + t, 2 * unit + t + count)
+                spread_bias = bias_rows[:].unsqueeze(1).to_broadcast([P, count, N])
+                sums = acts[:, 2 * unit - 2 + t : 2 * unit - 2 + t + count, :]
+                nc.vector.tensor_tensor(sums, both[unit][:, t : t + count, :], spread_bias, ADD)
+                nc.scalar.activation(staged[:, rows, :], sums, SILU)
             leave_upright(unit)
         for t in range(2):
             nc.vector.tensor_tensor(acts[:, 10 + t, :], ends[5, t], bias_rows[:], ADD)
             nc.scalar.activation(staged[:, 10 + t, :], acts[:, 10 + t, :], SILU)
-        leave_upright(5)
+            nc.sync.dma_start(out=out[P * (10 + t) : P * (11 + t), :], in_=staged[:, 10 + t, :])

from contextlib import ExitStack

import concourse.mybir as mybir
from concourse.masks import make_identity

K, L, N, T, S = 512, 2048, 128, 4096, 1536
FLOPS = 2 * S * N * (K + L)

F32 = mybir.dt.float32
BF16 = mybir.dt.bfloat16
I32 = mybir.dt.int32
U32 = mybir.dt.uint32
U16 = mybir.dt.uint16
U8 = mybir.dt.uint8
FP8X4 = mybir.dt.float8_e4m3fn_x4
FP4X4 = mybir.dt.float4_e2m1fn_x4
SILU = mybir.ActivationFunctionType.Silu
ADD = mybir.AluOpType.add

P = 128
WORD_BYTES = 512 * T
UNIT = 256
UNITS = S // UNIT
TURNED = 3
LIST_COLS = S // 16
QUADRANTS = (0, 2, 1, 3)

EDGE = 128
WINDOW2_AT = 4 * T - EDGE
WINDOW1_AT = WINDOW2_AT + T
W_SCALES_AT = WINDOW2_AT + EDGE
PLANES2_AT = W_SCALES_AT + N
PLANE1_AT = PLANES2_AT + 4 * S
TAB_WORDS_AT = WINDOW1_AT + T - EDGE


def tile_list_tab48_tm_silu_kernel(tc, tab, w4_words, w4_scales, tab2, u, b, offs, offs2, out):
    nc = tc.nc
    with ExitStack() as ctx:
        lists = ctx.enter_context(tc.tile_pool(name="lists", bufs=1))
        keep = ctx.enter_context(tc.tile_pool(name="keep", bufs=1))
        shared = ctx.enter_context(tc.tile_pool(name="shared", bufs=1))
        psum = ctx.enter_context(tc.psum_pool(name="psum", bufs=1))

        def load_words(tile, row):
            nc.sync.dma_start(out=tile[:], in_=row[:, :WORD_BYTES].bitcast(I32).rearrange("o (p t) -> (o p) t", p=P))

        def gather(dst, window, offsets, first, count):
            nc.vector.tensor_copy(dst, window.indirect(offsets[:, first // 16 : (first + count) // 16]))

        def part(parted, pairs, first, count):
            cols = slice(first, first + count)
            nc.vector.tensor_copy(
                parted[:].bitcast(U16).rearrange("p (h j) -> p h j", h=2)[:, :, cols],
                pairs[:].bitcast(U16).rearrange("p (j h) -> p h j", h=2)[:, :, cols],
            )

        list2 = lists.tile([P, LIST_COLS], U16, name="list2")
        list1 = lists.tile([P, LIST_COLS], U16, name="list1")
        window2 = shared.tile([P, T // 4], I32, name="window2", offset=WINDOW2_AT, align_bytes=64)
        window1 = shared.tile([P, T // 4], I32, name="window1", offset=WINDOW1_AT, align_bytes=64)

        nc.vector.memset(window1[:], 0)
        nc.vector.memset(window2[0:32, :], 0)
        nc.vector.memset(window2[96:128, :], 0)
        ident = keep.tile([P, P], F32, name="ident")
        nc.vector.memset(ident[:], 0.0)
        make_identity(nc, ident[:], nomemset=True)

        nc.sync.dma_start(list2[:], offs2)
        for m in range(2):
            nc.sync.dma_start(
                out=window2[32 + m : 96 : 2, :],
                in_=tab2[m : m + 1, WORD_BYTES:].bitcast(I32).rearrange("o (h q c) -> (o q) h c", h=2, q=16),
            )
        nc.sync.dma_start(list1[:], offs)
        nc.sync.dma_start(
            out=window1[32:96:4, :], in_=tab[0:1, WORD_BYTES:].bitcast(I32).rearrange("o (q c) -> (o q) c", c=T // 4)
        )
        w_codes = keep.tile([P, 2 * N], U8, name="w_codes", align_bytes=256)
        nc.sync.dma_start(out=w_codes[:].bitcast(I32), in_=w4_words[0].bitcast(I32))
        bias = keep.tile([P, 1], F32, name="bias")
        nc.sync.dma_start(out=bias[:], in_=b.rearrange("(p o) -> p o", o=1))
        pair0_words = keep.tile([P, T], I32, name="pair0_words", align_bytes=256)
        load_words(pair0_words, tab2[0:1])
        u_rows = keep.tile([P, 4, 4, N], F32, name="u_rows", align_bytes=256)
        nc.sync.dma_start(
            out=u_rows[:].rearrange("p a i n -> p a (i n)"), in_=u.rearrange("(a p i) n -> p a (i n)", a=4, i=4)
        )

        scales2 = keep.tile([P, S], U8, name="scales2", align_bytes=64)
        gather(scales2[:], window2[:].bitcast(U8), list2, 0, S)
        w_scales = shared.tile([P, N], U8, name="w_scales", offset=W_SCALES_AT, align_bytes=64)
        planes2 = [
            shared.tile([P, 2 * S], U8, name=f"planes2_{m}", offset=PLANES2_AT + 2 * S * m, align_bytes=64)
            for m in range(2)
        ]
        plane1 = shared.tile([P, S], U8, name="plane1", offset=PLANE1_AT, align_bytes=64)

        def load_w_scales(quads):
            for quad in quads:
                nc.sync.dma_start(
                    out=w_scales[32 * quad : 32 * quad + 4, :].bitcast(I32),
                    in_=w4_scales[0, 4 * quad : 4 * quad + 4, :].bitcast(I32),
                )

        def move_tab2_rows(m):
            for quad in QUADRANTS:
                nc.sync.dma_start(
                    out=planes2[m][32 * quad : 32 * quad + 4, :].bitcast(I32).rearrange("r (h c) -> r h c", h=2),
                    in_=scales2[32 + 16 * quad + m : 48 + 16 * quad : 2, :].bitcast(I32),
                )

        def move_tab_rows(quad, first, last):
            nc.sync.dma_start(
                out=plane1[32 * quad : 32 * quad + 4, first:last].bitcast(I32),
                in_=scales1[32 + 16 * quad : 48 + 16 * quad : 4, first:last].bitcast(I32),
            )

        move_tab2_rows(0)
        load_w_scales(QUADRANTS[:2])
        pair1_words = shared.tile([P, T], I32, name="pair1_words", offset=0, align_bytes=256)
        load_words(pair1_words, tab2[1:2])
        scales1 = keep.tile([P, S], U8, name="scales1", align_bytes=64)
        gather(scales1[:], window1[:].bitcast(U8), list1, 0, S)
        move_tab2_rows(1)
        load_w_scales(QUADRANTS[2:])
        tab_words = shared.tile([P, T], I32, name="tab_words", offset=TAB_WORDS_AT, align_bytes=256)
        load_words(tab_words, tab[0:1])
        move_tab_rows(QUADRANTS[0], 0, S)
        for quad in QUADRANTS[1:3]:
            move_tab_rows(quad, 0, 4 * UNIT)
        for first, last in ((0, 1), (1, 3), (3, 4)):
            move_tab_rows(QUADRANTS[3], UNIT * first, UNIT * last)
        for quad in QUADRANTS[1:3]:
            move_tab_rows(quad, 4 * UNIT, S)
        for unit in (4, 5):
            move_tab_rows(QUADRANTS[3], UNIT * unit, UNIT * (unit + 1))

        u_grouped = keep.tile([P, 4, N, 4], BF16, name="u_grouped", align_bytes=64)
        nc.scalar.copy(out=u_grouped[:], in_=u_rows[:].rearrange("p a i n -> p a n i"))

        u_codes = keep.tile([P, 4 * N], U32, name="u_codes", align_bytes=64)
        u_scales = keep.tile([P, 4 * N], U8, name="u_scales", align_bytes=64)

        spread = psum.tile([P, N], F32, name="spread", tag="spare")
        nc.tensor.transpose(spread[:], bias[:].to_broadcast([P, P]), ident[:])
        bias_rows = keep.tile([P, N], F32, name="bias_rows")
        nc.scalar.copy(bias_rows[:], spread[:])

        acc = [psum.tile([P, UNIT], F32, name=f"acc{g}", tag=f"acc{g}") for g in range(TURNED)]
        both = {g: psum.tile([P, 2, N], F32, name=f"both{g}", tag=f"both{g}") for g in range(TURNED, UNITS - 1)}
        last = [psum.tile([P, N], F32, name=f"end{t}", tag=f"end{t}") for t in range(2)]
        ends = {(g, t): both[g][:, t, :] for g in both for t in range(2)}
        for t in range(2):
            ends[UNITS - 1, t] = last[t][:]
        pairs = [keep.tile([P, S], U32, name=f"pairs{m}", align_bytes=64) for m in range(2)]
        parted = [keep.tile([P, 4 * S], U8, name=f"parted{m}", align_bytes=64) for m in range(2)]

        def multiply(unit, codes, width, scales, w, w_scale, fmt, w_fmt, start, stop):
            if unit < TURNED:
                nc.tensor.matmul_mx(
                    out=acc[unit][:], lhsT=w.bitcast(w_fmt), lhsT_scale=w_scale, rhs=codes.bitcast(fmt),
                    rhs_scale=scales, start=start, stop=stop,
                )
            else:
                for t in range(2):
                    nc.tensor.matmul_mx(
                        out=ends[unit, t], lhsT=codes[:, width * P * t : width * P * (t + 1)].bitcast(fmt),
                        lhsT_scale=scales[:, P * t : P * (t + 1)], rhs=w.bitcast(w_fmt), rhs_scale=w_scale,
                        start=start and (unit == 5 or t == 0), stop=stop and (unit == 5 or t == 1),
                    )

        def tab2_passes(m, first, count):
            for h in range(2):
                cols = slice(N * (2 * m + h), N * (2 * m + h + 1))
                for item in range(first, first + count, UNIT):
                    codes = parted[m][:, 2 * (S * h + item) : 2 * (S * h + item + UNIT)]
                    scales = planes2[m][:, S * h + item : S * h + item + UNIT]
                    multiply(
                        item // UNIT, codes, 2, scales, u_codes[:, cols], u_scales[:, cols], FP4X4, FP8X4,
                        m == 0 and h == 0, False,
                    )

        for first in (0, S // 2):
            gather(pairs[0][:, first : first + S // 2], pair0_words[:].bitcast(U32), list2, first, S // 2)
        for first in (0, S // 2):
            part(parted[0], pairs[0], first, S // 2)
        nc.vector.quantize_mx(
            out=u_codes[:].bitcast(FP8X4), scales=u_scales[:], in_=u_grouped[:].rearrange("p a n i -> p (a n i)")
        )
        tab2_passes(0, 0, S)

        third = S // 3
        for step in range(4):
            if step < 3:
                first = third * step
                gather(pairs[1][:, first : first + third], pair1_words[:].bitcast(U32), list2, first, third)
            if step > 0:
                first = third * (step - 1)
                part(parted[1], pairs[1], first, third)
                tab2_passes(1, first, third)

        acts = keep.tile([P, S // P, P], F32, name="acts")
        staged = keep.tile([P, S // P, N], F32, name="staged")

        def close(unit):
            codes = keep.tile([P, UNIT], U32, name=f"tab_codes{unit}", align_bytes=64)
            gather(codes[:], tab_words[:].bitcast(U32), list1, UNIT * unit, UNIT)
            cols = slice(UNIT * unit, UNIT * (unit + 1))
            multiply(unit, codes[:], 1, plane1[:, cols], w_codes[:], w_scales[:], FP8X4, FP4X4, False, True)

        def activate(unit, t, count):
            dealt = acc[unit][:].rearrange("n (p t) -> n t p", p=P)
            rows = slice(2 * unit + t, 2 * unit + t + count)
            nc.scalar.activation(acts[:, rows, :], dealt[:, t : t + count, :], SILU, bias=bias[:])

        def turn(first, count, bank):
            turned = psum.tile([P, count, N], F32, name=f"turned{first}", tag=bank)
            for t in range(count):
                nc.tensor.transpose(turned[:, t, :], acts[:, first + t, :], ident[:])
            return turned

        def store(unit):
            rows = out[UNIT * unit : UNIT * (unit + 1), :].rearrange("(p t) n -> p t n", p=P)
            nc.sync.dma_start(out=rows, in_=staged[:, 2 * unit : 2 * unit + 2, :])

        def leave(unit, copy):
            copy(staged[:, 2 * unit : 2 * unit + 2, :], turned[unit][:])
            store(unit)

        def leave_upright(unit):
            rows = out[UNIT * unit : UNIT * (unit + 1), :].rearrange("(t p) n -> p t n", p=P)
            nc.sync.dma_start(out=rows, in_=staged[:, 2 * unit : 2 * unit + 2, :])

        turned = {}
        banks = ("spare", "acc0", "acc1")
        for unit in range(UNITS):
            close(unit)
        for unit in range(TURNED):
            activate(unit, 0, 2)
            turned[unit] = turn(2 * unit, 2, banks[unit])
        for unit in range(TURNED):
            leave(unit, nc.scalar.copy)
        for unit in range(TURNED, UNITS - 1):
            for t, count in ((0, 1), (1, 1)) if unit == TURNED else ((0, 2),):
                rows = slice(2 * unit + t, 2 * unit + t + count)
                spread_bias = bias_rows[:].unsqueeze(1).to_broadcast([P, count, N])
                sums = acts[:, 2 * unit - 2 + t : 2 * unit - 2 + t + count, :]
                nc.vector.tensor_tensor(sums, both[unit][:, t : t + count, :], spread_bias, ADD)
                nc.scalar.activation(staged[:, rows, :], sums, SILU)
            leave_upright(unit)
        for t in range(2):
            nc.vector.tensor_tensor(acts[:, 10 + t, :], ends[5, t], bias_rows[:], ADD)
            nc.scalar.activation(staged[:, 10 + t, :], acts[:, 10 + t, :], SILU)
            nc.sync.dma_start(out=out[P * (10 + t) : P * (11 + t), :], in_=staged[:, 10 + t, :])
